import numpy as np
import ml_dtypes


def mxq(x, axis, fmt="e4m3"):
    dtype, down = {"e4m3": (ml_dtypes.float8_e4m3fn, 7), "e5m2": (ml_dtypes.float8_e5m2, 14)}[fmt]
    v = np.moveaxis(np.asarray(x, np.float32).astype(ml_dtypes.bfloat16).astype(np.float64), axis, -1)
    blocks = v.reshape(v.shape[:-1] + (-1, 32))
    amax = np.abs(blocks).max(-1, keepdims=True)
    byte = np.maximum(np.where(amax > 0, np.frexp(amax)[1] - 1 + 127, 0) - down, 1)
    scale = np.exp2(byte - 127.0)
    codes = (blocks / scale).astype(np.float32).astype(dtype).astype(np.float64)
    return np.moveaxis((codes * scale).reshape(v.shape), -1, axis)


WIDE = False


def mx_kscale(k):
    if not WIDE:
        return np.ones(k)
    levels = np.array([10, -10, 5, -5, 0])
    if k % 512:
        return np.exp2(np.random.permutation(np.resize(levels, k // 32))).repeat(32)
    a = np.empty((k // 512, 16))
    for p in range(k // 512):
        a[p, :8] = np.random.permutation(np.resize(levels, 8))
        for g in range(8):
            far = levels[np.abs(levels - a[p, g]) >= 10]
            a[p, g + 8] = far[np.random.randint(len(far))]
    return np.exp2(a.ravel()).repeat(32)


def f64(x):
    return np.asarray(x).astype(np.float64)


def striped(idx):
    return np.tile(idx.reshape(-1, 16).T, (8, 1)).astype(np.uint16)


def unstriped(offs):
    return offs[:16].T.reshape(-1).astype(np.int64)


K, T, S, V, N = 512, 4096, 2048, 512, 256


def setup_inputs():
    n = np.random.standard_normal
    s = mx_kscale(K)[:, None]
    return {
        "xT": (n((K, T)) * s).astype(np.float32),
        "w1": (n((K, N)) / np.sqrt(K) / s).astype(np.float32),
        "offs": striped(np.random.permutation(T)[:S]),
    }


def reference(xT, w1, offs):
    xq = mxq(f64(xT)[:, unstriped(offs)], 0, "e4m3")
    e = np.exp(mxq(f64(w1), 0, "e4m3").T @ xq)
    return np.log(e[:, :V] + e[:, V:2 * V] + e[:, 2 * V:3 * V] + e[:, 3 * V:4 * V])

@@ -1,0 +1,155 @@
+from contextlib import ExitStack
+
+import concourse.mybir as mybir
+from concourse.masks import make_identity
+
+K, T, S, V, N = 512, 4096, 2048, 512, 256
+D = S // V
+FLOPS = 2 * K * N * S
+
+F32 = mybir.dt.float32
+BF16 = mybir.dt.bfloat16
+U32 = mybir.dt.uint32
+U16 = mybir.dt.uint16
+U8 = mybir.dt.uint8
+FP8X4 = mybir.dt.float8_e4m3fn_x4
+ALU = mybir.AluOpType
+ACT = mybir.ActivationFunctionType
+
+P = 128
+PACK = 4
+M_TILES = N // P
+CHUNKS = (2048, 1024, 768, 256)
+W_AFTER = 0
+HALVES = 2
+HALF = V // HALVES
+GATHERS = (("vector", 0, 768), ("scalar", 768, 768), ("scalar", 1536, 512))
+
+
+def tile_picked_lsep_none_e_kernel(tc, xT, w1, offs, out):
+    nc = tc.nc
+    with ExitStack() as ctx:
+        keep = ctx.enter_context(tc.tile_pool(name="keep", bufs=1))
+        psum = ctx.enter_context(tc.psum_pool(name="psum", bufs=1))
+
+        offsets = keep.tile([P, S // 16], U16, name="offsets")
+        nc.sync.dma_start(offsets[:], offs)
+
+        identity = keep.tile([P, P], F32, name="identity")
+        make_identity(nc, identity[:])
+
+        w_raw = keep.tile([P, PACK, N], F32, name="w_raw")
+        w_grouped = keep.tile([P, N, PACK], BF16, name="w_grouped", align_bytes=64)
+        w_codes = keep.tile([P, N], U32, name="w_codes", align_bytes=64)
+        w_scales = keep.tile([P, N], U8, name="w_scales", align_bytes=64)
+
+        x_rows = xT.rearrange("(p j) t -> p j t", j=PACK)
+        picked = [
+            keep.tile([P, count, PACK], BF16, name="picked%d" % g, align_bytes=64)
+            for g, (engine, first, count) in enumerate(GATHERS)
+        ]
+        for j in range(PACK):
+            plane = keep.tile([P, T], F32, name="plane%d" % j)
+            rounded = keep.tile([P, T], BF16, name="rounded%d" % j)
+            c0 = 0
+            for width in CHUNKS:
+                cols = slice(c0, c0 + width)
+                c0 = c0 + width
+                nc.sync.dma_start(out=plane[:, cols], in_=x_rows[:, j, cols])
+                if c0 == T:
+                    nc.scalar.copy(out=rounded[:, cols], in_=plane[:, cols])
+                else:
+                    nc.vector.tensor_copy(out=rounded[:, cols], in_=plane[:, cols])
+            if j == W_AFTER:
+                nc.sync.dma_start(out=w_raw[:], in_=w1.rearrange("(p j) n -> p j n", j=PACK))
+            for g, (engine, first, count) in enumerate(GATHERS):
+                entries = offsets[:, first // 16 : (first + count) // 16]
+                if engine == "vector":
+                    nc.vector.tensor_copy(picked[g][:, :, j], plane[:].indirect(entries))
+                else:
+                    nc.scalar.activation(picked[g][:, :, j], rounded[:].indirect(entries), ACT.Copy)
+            if j == W_AFTER:
+                nc.vector.tensor_copy(out=w_grouped[:], in_=w_raw[:].rearrange("p j n -> p n j"))
+                nc.vector.quantize_mx(
+                    out=w_codes[:].bitcast(FP8X4),
+                    scales=w_scales[:],
+                    in_=w_grouped[:].rearrange("p n j -> p (n j)"),
+                )
+
+        codes = [keep.tile([P, V], U32, name="codes%d" % d, align_bytes=64) for d in range(D)]
+        scales = [keep.tile([P, V], U8, name="scales%d" % d, align_bytes=64) for d in range(D)]
+        y = {}
+        for d in range(D):
+            for g, (engine, first, count) in enumerate(GATHERS):
+                lo = max(first, d * V)
+                hi = min(first + count, (d + 1) * V)
+                if lo < hi:
+                    nc.vector.quantize_mx(
+                        out=codes[d][:, lo - d * V : hi - d * V].bitcast(FP8X4),
+                        scales=scales[d][:, lo - d * V : hi - d * V],
+                        in_=picked[g][:, lo - first : hi - first, :].rearrange("p n j -> p (n j)"),
+                    )
+            for h in range(HALVES):
+                y[d, h] = psum.tile([P, HALF // P, N], F32, name="y%d_%d" % (d, h), tag="bank%d_%d" % (d, h))
+                for b in range(HALF // P):
+                    cols = slice(h * HALF + b * P, h * HALF + (b + 1) * P)
+                    nc.tensor.matmul_mx(
+                        out=y[d, h][:, b, :],
+                        lhsT=codes[d][:, cols].bitcast(FP8X4),
+                        lhsT_scale=scales[d][:, cols],
+                        rhs=w_codes[:].bitcast(FP8X4),
+                        rhs_scale=w_scales[:],
+                        start=True,
+                        stop=True,
+                    )
+
+        largest = {}
+        for h in range(HALVES):
+            largest[0, h] = keep.tile([P, HALF // P, N], F32, name="largest0_%d" % h)
+            nc.scalar.copy(out=largest[0, h][:], in_=y[0, h][:])
+        for d in range(1, D):
+            for h in range(HALVES):
+                largest[d, h] = keep.tile([P, HALF // P, N], F32, name="largest%d_%d" % (d, h))
+                nc.vector.tensor_tensor(largest[d, h][:], y[d, h][:], largest[d - 1, h][:], ALU.max)
+
+        blocks = [(b, t) for b in range(HALF // P) for t in range(M_TILES)]
+        order = (1, 0, 2, 3)
+        shifts = []
+        totals = []
+        for h in range(HALVES):
+            top = largest[D - 1, h]
+            shift = psum.tile([P, M_TILES, HALF], F32, name="shift%d" % h, tag="bank0_%d" % h)
+            shifts.append(shift)
+            for b, t in blocks:
+                nc.tensor.transpose(shift[:, t, b * P : (b + 1) * P], top[:, b, t * P : (t + 1) * P], identity[:])
+            terms = []
+            for d in order:
+                below = keep.tile([P, HALF // P, N], F32, name="below%d_%d" % (d, h), tag="below%d_%d" % (d, h))
+                source = largest[0, h] if d == 0 else y[d, h]
+                nc.vector.tensor_tensor(below[:], source[:], top[:], ALU.subtract)
+                term = keep.tile([P, HALF // P, N], F32, name="term%d_%d" % (d, h))
+                nc.scalar.activation(term[:], below[:], ACT.Exp)
+                terms.append(term)
+            total = psum.tile([P, M_TILES, HALF], F32, name="total%d" % h, tag="bank1_%d" % h)
+            totals.append(total)
+            for i, term in enumerate(terms):
+                for b, t in blocks:
+                    nc.tensor.matmul(
+                        total[:, t, b * P : (b + 1) * P],
+                        term[:, b, t * P : (t + 1) * P],
+                        identity[:],
+                        start=(i == 0 and (b, t) == blocks[0]),
+                        stop=(i == D - 1 and (b, t) == blocks[-1]),
+                        is_transpose=True,
+                    )
+
+        logs = []
+        for h in range(HALVES):
+            log_tile = keep.tile([P, M_TILES, HALF], F32, name="logs%d" % h, tag="below%d_%d" % (order[-1 - h], HALVES - 1))
+            logs.append(log_tile)
+        for h in range(HALVES):
+            for t in range(M_TILES):
+                nc.scalar.activation(logs[h][:, t, :], totals[h][:, t, :], ACT.Ln)
+                result = keep.tile([P, HALF], F32, name="result%d_%d" % (h, t))
+                nc.vector.tensor_tensor(result[:], shifts[h][:, t, :], logs[h][:, t, :], ALU.add)
+                nc.sync.dma_start(out=out[t * P : (t + 1) * P, h * HALF : (h + 1) * HALF], in_=result[:])

@@ -10,6 +10,7 @@ FLOPS = 2 * K * N * S
 F32 = mybir.dt.float32
 BF16 = mybir.dt.bfloat16
 U32 = mybir.dt.uint32
+I32 = mybir.dt.int32
 U16 = mybir.dt.uint16
 U8 = mybir.dt.uint8
 FP8X4 = mybir.dt.float8_e4m3fn_x4
@@ -23,7 +24,7 @@ CHUNKS = (2048, 1024, 768, 256)
 W_AFTER = 0
 HALVES = 2
 HALF = V // HALVES
-GATHERS = (("vector", 0, 768), ("scalar", 768, 768), ("scalar", 1536, 512))
+WOVEN = (1, 2)
 
 
 def tile_picked_lsep_none_e_kernel(tc, xT, w1, offs, out):
@@ -44,10 +45,8 @@ def tile_picked_lsep_none_e_kernel(tc, xT, w1, offs, out):
         w_scales = keep.tile([P, N], U8, name="w_scales", align_bytes=64)
 
         x_rows = xT.rearrange("(p j) t -> p j t", j=PACK)
-        picked = [
-            keep.tile([P, count, PACK], BF16, name="picked%d" % g, align_bytes=64)
-            for g, (engine, first, count) in enumerate(GATHERS)
-        ]
+        picked = [keep.tile([P, V, PACK], BF16, name="picked%d" % d, align_bytes=64) for d in range(D)]
+        pairs = {d: keep.tile([P, 2, V, 2], BF16, name="pairs%d" % d) for d in WOVEN}
         for j in range(PACK):
             plane = keep.tile([P, T], F32, name="plane%d" % j)
             rounded = keep.tile([P, T], BF16, name="rounded%d" % j)
@@ -56,18 +55,16 @@ def tile_picked_lsep_none_e_kernel(tc, xT, w1, offs, out):
                 cols = slice(c0, c0 + width)
                 c0 = c0 + width
                 nc.sync.dma_start(out=plane[:, cols], in_=x_rows[:, j, cols])
-                if c0 == T:
-                    nc.scalar.copy(out=rounded[:, cols], in_=plane[:, cols])
-                else:
-                    nc.vector.tensor_copy(out=rounded[:, cols], in_=plane[:, cols])
+                nc.vector.tensor_copy(out=rounded[:, cols], in_=plane[:, cols])
             if j == W_AFTER:
                 nc.sync.dma_start(out=w_raw[:], in_=w1.rearrange("(p j) n -> p j n", j=PACK))
-            for g, (engine, first, count) in enumerate(GATHERS):
-                entries = offsets[:, first // 16 : (first + count) // 16]
-                if engine == "vector":
-                    nc.vector.tensor_copy(picked[g][:, :, j], plane[:].indirect(entries))
+            for d in range(D):
+                entries = offsets[:, d * V // 16 : (d + 1) * V // 16]
+                slot = pairs[d][:, j // 2, :, j % 2] if d in WOVEN else picked[d][:, :, j]
+                if d == 0:
+                    nc.vector.tensor_copy(slot, plane[:].indirect(entries))
                 else:
-                    nc.scalar.activation(picked[g][:, :, j], rounded[:].indirect(entries), ACT.Copy)
+                    nc.scalar.activation(slot, rounded[:].indirect(entries), ACT.Copy)
             if j == W_AFTER:
                 nc.vector.tensor_copy(out=w_grouped[:], in_=w_raw[:].rearrange("p j n -> p n j"))
                 nc.vector.quantize_mx(
@@ -76,27 +73,28 @@ def tile_picked_lsep_none_e_kernel(tc, xT, w1, offs, out):
                     in_=w_grouped[:].rearrange("p n j -> p (n j)"),
                 )
 
-        codes = [keep.tile([P, V], U32, name="codes%d" % d, align_bytes=64) for d in range(D)]
-        scales = [keep.tile([P, V], U8, name="scales%d" % d, align_bytes=64) for d in range(D)]
         y = {}
-        for d in range(D):
-            for g, (engine, first, count) in enumerate(GATHERS):
-                lo = max(first, d * V)
-                hi = min(first + count, (d + 1) * V)
-                if lo < hi:
-                    nc.vector.quantize_mx(
-                        out=codes[d][:, lo - d * V : hi - d * V].bitcast(FP8X4),
-                        scales=scales[d][:, lo - d * V : hi - d * V],
-                        in_=picked[g][:, lo - first : hi - first, :].rearrange("p n j -> p (n j)"),
-                    )
+
+        def weave(d):
+            nc.vector.tensor_copy(
+                out=picked[d][:].rearrange("p n j -> p (n j)").bitcast(I32).rearrange("p (n u) -> p n u", u=2),
+                in_=pairs[d][:].rearrange("p u n e -> p u (n e)").bitcast(I32).rearrange("p u n -> p n u"),
+            )
+
+        def multiply(d):
+            codes = keep.tile([P, V], U32, name="codes%d" % d, align_bytes=64)
+            scales = keep.tile([P, V], U8, name="scales%d" % d, align_bytes=64)
+            nc.vector.quantize_mx(
+                out=codes[:].bitcast(FP8X4), scales=scales[:], in_=picked[d][:].rearrange("p n j -> p (n j)")
+            )
             for h in range(HALVES):
                 y[d, h] = psum.tile([P, HALF // P, N], F32, name="y%d_%d" % (d, h), tag="bank%d_%d" % (d, h))
                 for b in range(HALF // P):
                     cols = slice(h * HALF + b * P, h * HALF + (b + 1) * P)
                     nc.tensor.matmul_mx(
                         out=y[d, h][:, b, :],
-                        lhsT=codes[d][:, cols].bitcast(FP8X4),
-                        lhsT_scale=scales[d][:, cols],
+                        lhsT=codes[:, cols].bitcast(FP8X4),
+                        lhsT_scale=scales[:, cols],
                         rhs=w_codes[:].bitcast(FP8X4),
                         rhs_scale=w_scales[:],
                         start=True,
@@ -104,52 +102,79 @@ def tile_picked_lsep_none_e_kernel(tc, xT, w1, offs, out):
                     )
 
         largest = {}
-        for h in range(HALVES):
-            largest[0, h] = keep.tile([P, HALF // P, N], F32, name="largest0_%d" % h)
-            nc.scalar.copy(out=largest[0, h][:], in_=y[0, h][:])
-        for d in range(1, D):
-            for h in range(HALVES):
-                largest[d, h] = keep.tile([P, HALF // P, N], F32, name="largest%d_%d" % (d, h))
-                nc.vector.tensor_tensor(largest[d, h][:], y[d, h][:], largest[d - 1, h][:], ALU.max)
-
+        copies = {}
+        shifts = {}
+        terms = {}
+        totals = {}
         blocks = [(b, t) for b in range(HALF // P) for t in range(M_TILES)]
-        order = (1, 0, 2, 3)
-        shifts = []
-        totals = []
-        for h in range(HALVES):
-            top = largest[D - 1, h]
-            shift = psum.tile([P, M_TILES, HALF], F32, name="shift%d" % h, tag="bank0_%d" % h)
-            shifts.append(shift)
+
+        def copy_out(d, h):
+            copies[d, h] = keep.tile([P, HALF // P, N], F32, name="copy%d_%d" % (d, h))
+            nc.scalar.copy(out=copies[d, h][:], in_=y[d, h][:])
+
+        def running_max(d, h):
+            before = copies[0, h] if d == 1 else largest[d - 1, h]
+            largest[d, h] = keep.tile([P, HALF // P, N], F32, name="largest%d_%d" % (d, h))
+            nc.vector.tensor_tensor(largest[d, h][:], y[d, h][:], before[:], ALU.max)
+
+        def turn_largest(h):
+            shifts[h] = psum.tile([P, M_TILES, HALF], F32, name="shift%d" % h, tag="bank0_%d" % h)
             for b, t in blocks:
-                nc.tensor.transpose(shift[:, t, b * P : (b + 1) * P], top[:, b, t * P : (t + 1) * P], identity[:])
-            terms = []
-            for d in order:
-                below = keep.tile([P, HALF // P, N], F32, name="below%d_%d" % (d, h), tag="below%d_%d" % (d, h))
-                source = largest[0, h] if d == 0 else y[d, h]
-                nc.vector.tensor_tensor(below[:], source[:], top[:], ALU.subtract)
-                term = keep.tile([P, HALF // P, N], F32, name="term%d_%d" % (d, h))
-                nc.scalar.activation(term[:], below[:], ACT.Exp)
-                terms.append(term)
-            total = psum.tile([P, M_TILES, HALF], F32, name="total%d" % h, tag="bank1_%d" % h)
-            totals.append(total)
-            for i, term in enumerate(terms):
+                nc.tensor.transpose(
+                    shifts[h][:, t, b * P : (b + 1) * P], largest[D - 1, h][:, b, t * P : (t + 1) * P], identity[:]
+                )
+
+        def exponential(d, h, engine):
+            below = keep.tile([P, HALF // P, N], F32, name="below%d_%d" % (d, h), tag="below%d_%d" % (d, h))
+            source = copies[d, h] if (d, h) in copies else y[d, h]
+            engine.tensor_tensor(below[:], source[:], largest[D - 1, h][:], ALU.subtract)
+            terms[d, h] = keep.tile([P, HALF // P, N], F32, name="term%d_%d" % (d, h))
+            nc.scalar.activation(terms[d, h][:], below[:], ACT.Exp)
+
+        def add_up(h, order):
+            totals[h] = psum.tile([P, M_TILES, HALF], F32, name="total%d" % h, tag="bank1_%d" % h)
+            for i, d in enumerate(order):
                 for b, t in blocks:
                     nc.tensor.matmul(
-                        total[:, t, b * P : (b + 1) * P],
-                        term[:, b, t * P : (t + 1) * P],
+                        totals[h][:, t, b * P : (b + 1) * P],
+                        terms[d, h][:, b, t * P : (t + 1) * P],
                         identity[:],
                         start=(i == 0 and (b, t) == blocks[0]),
                         stop=(i == D - 1 and (b, t) == blocks[-1]),
                         is_transpose=True,
                     )
 
-        logs = []
+        weave(1)
+        multiply(0)
+        multiply(1)
+        weave(2)
+        multiply(2)
+        multiply(3)
+        copy_out(0, 0)
+        copy_out(0, 1)
+        running_max(1, 0)
+        running_max(2, 0)
+        running_max(3, 0)
+        turn_largest(0)
+        exponential(0, 0, nc.gpsimd)
+        running_max(1, 1)
+        exponential(1, 0, nc.vector)
+        running_max(2, 1)
+        exponential(2, 0, nc.vector)
+        running_max(3, 1)
+        turn_largest(1)
+        exponential(3, 0, nc.vector)
+        exponential(1, 1, nc.vector)
+        exponential(0, 1, nc.gpsimd)
+        add_up(0, (0, 1, 2, 3))
+        exponential(2, 1, nc.vector)
+        exponential(3, 1, nc.vector)
+        add_up(1, (1, 0, 2, 3))
+
         for h in range(HALVES):
-            log_tile = keep.tile([P, M_TILES, HALF], F32, name="logs%d" % h, tag="below%d_%d" % (order[-1 - h], HALVES - 1))
-            logs.append(log_tile)
-        for h in range(HALVES):
+            logs = keep.tile([P, M_TILES, HALF], F32, name="logs%d" % h, tag="below%d_%d" % (D - 1 - h, HALVES - 1))
             for t in range(M_TILES):
-                nc.scalar.activation(logs[h][:, t, :], totals[h][:, t, :], ACT.Ln)
+                nc.scalar.activation(logs[:, t, :], totals[h][:, t, :], ACT.Ln)
                 result = keep.tile([P, HALF], F32, name="result%d_%d" % (h, t))
-                nc.vector.tensor_tensor(result[:], shifts[h][:, t, :], logs[h][:, t, :], ALU.add)
+                nc.vector.tensor_tensor(result[:], shifts[h][:, t, :], logs[:, t, :], ALU.add)
                 nc.sync.dma_start(out=out[t * P : (t + 1) * P, h * HALF : (h + 1) * HALF], in_=result[:])

@@ -20,8 +20,8 @@ ACT = mybir.ActivationFunctionType
 P = 128
 PACK = 4
 M_TILES = N // P
-CHUNKS = (2048, 1024, 768, 256)
-W_AFTER = 0
+CHUNKS = ((1024, 2048, 1024), (3072, 1024), (2560, 1024, 512), (2048, 1280, 512, 256))
+W_AFTER = 2
 HALVES = 2
 HALF = V // HALVES
 WOVEN = (1, 2)
@@ -34,7 +34,6 @@ def tile_picked_lsep_none_e_kernel(tc, xT, w1, offs, out):
         psum = ctx.enter_context(tc.psum_pool(name="psum", bufs=1))
 
         offsets = keep.tile([P, S // 16], U16, name="offsets")
-        nc.sync.dma_start(offsets[:], offs)
 
         identity = keep.tile([P, P], F32, name="identity")
         make_identity(nc, identity[:])
@@ -45,20 +44,26 @@ def tile_picked_lsep_none_e_kernel(tc, xT, w1, offs, out):
         w_scales = keep.tile([P, N], U8, name="w_scales", align_bytes=64)
 
         x_rows = xT.rearrange("(p j) t -> p j t", j=PACK)
-        picked = [keep.tile([P, V, PACK], BF16, name="picked%d" % d, align_bytes=64) for d in range(D)]
+        picked = {d: keep.tile([P, V, PACK], BF16, name="picked%d" % d, align_bytes=64) for d in range(D) if d not in WOVEN}
         pairs = {d: keep.tile([P, 2, V, 2], BF16, name="pairs%d" % d) for d in WOVEN}
         for j in range(PACK):
             plane = keep.tile([P, T], F32, name="plane%d" % j)
             rounded = keep.tile([P, T], BF16, name="rounded%d" % j)
             c0 = 0
-            for width in CHUNKS:
+            for width in CHUNKS[j]:
                 cols = slice(c0, c0 + width)
                 c0 = c0 + width
                 nc.sync.dma_start(out=plane[:, cols], in_=x_rows[:, j, cols])
-                nc.vector.tensor_copy(out=rounded[:, cols], in_=plane[:, cols])
+                if j == 0 and c0 == width:
+                    nc.scalar.copy(out=rounded[:, cols], in_=plane[:, cols])
+                else:
+                    nc.vector.tensor_copy(out=rounded[:, cols], in_=plane[:, cols])
+                if j == 0 and c0 == width:
+                    nc.sync.dma_start(offsets[:], offs)
             if j == W_AFTER:
                 nc.sync.dma_start(out=w_raw[:], in_=w1.rearrange("(p j) n -> p j n", j=PACK))
-            for d in range(D):
+            windows = (plane, rounded)
+            for d in range(D if j < PACK - 1 else D - 1):
                 entries = offsets[:, d * V // 16 : (d + 1) * V // 16]
                 slot = pairs[d][:, j // 2, :, j % 2] if d in WOVEN else picked[d][:, :, j]
                 if d == 0:
@@ -75,31 +80,44 @@ def tile_picked_lsep_none_e_kernel(tc, xT, w1, offs, out):
 
         y = {}
 
-        def weave(d):
+        def last_gather():
+            d = D - 1
+            entries = offsets[:, d * V // 16 : (d + 1) * V // 16]
+            nc.scalar.activation(picked[d][:, :, PACK - 1], windows[1][:].indirect(entries), ACT.Copy)
+
+        woven = {}
+
+        def weave(d, h, tag=None):
+            rows = slice(h * HALF, (h + 1) * HALF)
+            name = "woven%d_%d" % (d, h)
+            woven[d, h] = keep.tile([P, HALF, PACK], BF16, name=name, tag=tag or name, align_bytes=64)
+            words = pairs[d][:].rearrange("p u n e -> p u (n e)").bitcast(I32)
             nc.vector.tensor_copy(
-                out=picked[d][:].rearrange("p n j -> p (n j)").bitcast(I32).rearrange("p (n u) -> p n u", u=2),
-                in_=pairs[d][:].rearrange("p u n e -> p u (n e)").bitcast(I32).rearrange("p u n -> p n u"),
+                out=woven[d, h][:].rearrange("p n j -> p (n j)").bitcast(I32).rearrange("p (n u) -> p n u", u=2),
+                in_=words[:, :, rows].rearrange("p u n -> p n u"),
             )
 
-        def multiply(d):
-            codes = keep.tile([P, V], U32, name="codes%d" % d, align_bytes=64)
-            scales = keep.tile([P, V], U8, name="scales%d" % d, align_bytes=64)
+        def multiply(d, h, tag=None):
+            rows = slice(h * HALF, (h + 1) * HALF)
+            source = woven[d, h][:] if d in WOVEN else picked[d][:, rows, :]
+            name = "codes%d_%d" % (d, h)
+            codes = keep.tile([P, HALF], U32, name=name, tag=tag or name, align_bytes=64)
+            scales = keep.tile([P, HALF], U8, name="scales%d_%d" % (d, h), align_bytes=64)
             nc.vector.quantize_mx(
-                out=codes[:].bitcast(FP8X4), scales=scales[:], in_=picked[d][:].rearrange("p n j -> p (n j)")
+                out=codes[:].bitcast(FP8X4), scales=scales[:], in_=source.rearrange("p n j -> p (n j)")
             )
-            for h in range(HALVES):
-                y[d, h] = psum.tile([P, HALF // P, N], F32, name="y%d_%d" % (d, h), tag="bank%d_%d" % (d, h))
-                for b in range(HALF // P):
-                    cols = slice(h * HALF + b * P, h * HALF + (b + 1) * P)
-                    nc.tensor.matmul_mx(
-                        out=y[d, h][:, b, :],
-                        lhsT=codes[:, cols].bitcast(FP8X4),
-                        lhsT_scale=scales[:, cols],
-                        rhs=w_codes[:].bitcast(FP8X4),
-                        rhs_scale=w_scales[:],
-                        start=True,
-                        stop=True,
-                    )
+            y[d, h] = psum.tile([P, HALF // P, N], F32, name="y%d_%d" % (d, h), tag="bank%d_%d" % (d, h))
+            for b in range(HALF // P):
+                cols = slice(b * P, (b + 1) * P)
+                nc.tensor.matmul_mx(
+                    out=y[d, h][:, b, :],
+                    lhsT=codes[:, cols].bitcast(FP8X4),
+                    lhsT_scale=scales[:, cols],
+                    rhs=w_codes[:].bitcast(FP8X4),
+                    rhs_scale=w_scales[:],
+                    start=True,
+                    stop=True,
+                )
 
         largest = {}
         copies = {}
@@ -114,7 +132,8 @@ def tile_picked_lsep_none_e_kernel(tc, xT, w1, offs, out):
 
         def running_max(d, h):
             before = copies[0, h] if d == 1 else largest[d - 1, h]
-            largest[d, h] = keep.tile([P, HALF // P, N], F32, name="largest%d_%d" % (d, h))
+            name = "largest%d_%d" % (d, h)
+            largest[d, h] = keep.tile([P, HALF // P, N], F32, name=name, tag=name, align_bytes=64)
             nc.vector.tensor_tensor(largest[d, h][:], y[d, h][:], before[:], ALU.max)
 
         def turn_largest(h):
@@ -124,11 +143,12 @@ def tile_picked_lsep_none_e_kernel(tc, xT, w1, offs, out):
                     shifts[h][:, t, b * P : (b + 1) * P], largest[D - 1, h][:, b, t * P : (t + 1) * P], identity[:]
                 )
 
-        def exponential(d, h, engine):
+        def exponential(d, h, engine, tag=None):
             below = keep.tile([P, HALF // P, N], F32, name="below%d_%d" % (d, h), tag="below%d_%d" % (d, h))
             source = copies[d, h] if (d, h) in copies else y[d, h]
             engine.tensor_tensor(below[:], source[:], largest[D - 1, h][:], ALU.subtract)
-            terms[d, h] = keep.tile([P, HALF // P, N], F32, name="term%d_%d" % (d, h))
+            name = "term%d_%d" % (d, h)
+            terms[d, h] = keep.tile([P, HALF // P, N], F32, name=name, tag=tag or name)
             nc.scalar.activation(terms[d, h][:], below[:], ACT.Exp)
 
         def add_up(h, order):
@@ -144,29 +164,37 @@ def tile_picked_lsep_none_e_kernel(tc, xT, w1, offs, out):
                         is_transpose=True,
                     )
 
-        weave(1)
-        multiply(0)
-        multiply(1)
-        weave(2)
-        multiply(2)
-        multiply(3)
+        last_gather()
+        multiply(0, 0)
+        weave(1, 0)
+        multiply(0, 1)
+        multiply(1, 0)
+        weave(2, 0)
+        weave(1, 1)
+        multiply(2, 0)
+        multiply(1, 1)
+        multiply(3, 0)
         copy_out(0, 0)
         copy_out(0, 1)
         running_max(1, 0)
+        copy_out(1, 0)
+        weave(2, 1, "codes3_0")
         running_max(2, 0)
+        multiply(2, 1)
         running_max(3, 0)
+        multiply(3, 1, "largest1_0")
         turn_largest(0)
         exponential(0, 0, nc.gpsimd)
         running_max(1, 1)
-        exponential(1, 0, nc.vector)
-        running_max(2, 1)
         exponential(2, 0, nc.vector)
+        exponential(1, 0, nc.gpsimd, "below2_0")
+        running_max(2, 1)
+        exponential(3, 0, nc.vector)
         running_max(3, 1)
         turn_largest(1)
-        exponential(3, 0, nc.vector)
+        add_up(0, (0, 2, 1, 3))
         exponential(1, 1, nc.vector)
-        exponential(0, 1, nc.gpsimd)
-        add_up(0, (0, 1, 2, 3))
+        exponential(0, 1, nc.vector)
         exponential(2, 1, nc.vector)
         exponential(3, 1, nc.vector)
         add_up(1, (1, 0, 2, 3))

@@ -10,7 +10,6 @@ FLOPS = 2 * K * N * S
 F32 = mybir.dt.float32
 BF16 = mybir.dt.bfloat16
 U32 = mybir.dt.uint32
-I32 = mybir.dt.int32
 U16 = mybir.dt.uint16
 U8 = mybir.dt.uint8
 FP8X4 = mybir.dt.float8_e4m3fn_x4
@@ -20,11 +19,10 @@ ACT = mybir.ActivationFunctionType
 P = 128
 PACK = 4
 M_TILES = N // P
-CHUNKS = ((1024, 2048, 1024), (3072, 1024), (2560, 1024, 512), (2048, 1280, 512, 256))
-W_AFTER = 2
+BLOCKS = V // P
+LAST = D - 1
 HALVES = 2
 HALF = V // HALVES
-WOVEN = (1, 2)
 
 
 def tile_picked_lsep_none_e_kernel(tc, xT, w1, offs, out):
@@ -34,7 +32,6 @@ def tile_picked_lsep_none_e_kernel(tc, xT, w1, offs, out):
         psum = ctx.enter_context(tc.psum_pool(name="psum", bufs=1))
 
         offsets = keep.tile([P, S // 16], U16, name="offsets")
-
         identity = keep.tile([P, P], F32, name="identity")
         make_identity(nc, identity[:])
 
@@ -44,165 +41,169 @@ def tile_picked_lsep_none_e_kernel(tc, xT, w1, offs, out):
         w_scales = keep.tile([P, N], U8, name="w_scales", align_bytes=64)
 
         x_rows = xT.rearrange("(p j) t -> p j t", j=PACK)
-        picked = {d: keep.tile([P, V, PACK], BF16, name="picked%d" % d, align_bytes=64) for d in range(D) if d not in WOVEN}
-        pairs = {d: keep.tile([P, 2, V, 2], BF16, name="pairs%d" % d) for d in WOVEN}
+        nc.sync.dma_start(out=w_raw[:], in_=w1.rearrange("(p j) n -> p j n", j=PACK))
+        nc.scalar.copy(out=w_grouped[:], in_=w_raw[:].rearrange("p j n -> p n j"))
+        nc.vector.quantize_mx(
+            out=w_codes[:].bitcast(FP8X4), scales=w_scales[:], in_=w_grouped[:].rearrange("p n j -> p (n j)")
+        )
+        planes = []
         for j in range(PACK):
             plane = keep.tile([P, T], F32, name="plane%d" % j)
-            rounded = keep.tile([P, T], BF16, name="rounded%d" % j)
-            c0 = 0
-            for width in CHUNKS[j]:
-                cols = slice(c0, c0 + width)
-                c0 = c0 + width
-                nc.sync.dma_start(out=plane[:, cols], in_=x_rows[:, j, cols])
-                if j == 0 and c0 == width:
-                    nc.scalar.copy(out=rounded[:, cols], in_=plane[:, cols])
-                else:
-                    nc.vector.tensor_copy(out=rounded[:, cols], in_=plane[:, cols])
-                if j == 0 and c0 == width:
-                    nc.sync.dma_start(offsets[:], offs)
-            if j == W_AFTER:
-                nc.sync.dma_start(out=w_raw[:], in_=w1.rearrange("(p j) n -> p j n", j=PACK))
-            windows = (plane, rounded)
-            for d in range(D if j < PACK - 1 else D - 1):
-                entries = offsets[:, d * V // 16 : (d + 1) * V // 16]
-                slot = pairs[d][:, j // 2, :, j % 2] if d in WOVEN else picked[d][:, :, j]
-                if d == 0:
-                    nc.vector.tensor_copy(slot, plane[:].indirect(entries))
-                else:
-                    nc.scalar.activation(slot, rounded[:].indirect(entries), ACT.Copy)
-            if j == W_AFTER:
-                nc.vector.tensor_copy(out=w_grouped[:], in_=w_raw[:].rearrange("p j n -> p n j"))
-                nc.vector.quantize_mx(
-                    out=w_codes[:].bitcast(FP8X4),
-                    scales=w_scales[:],
-                    in_=w_grouped[:].rearrange("p n j -> p (n j)"),
-                )
+            planes.append(plane)
+            nc.sync.dma_start(out=plane[:], in_=x_rows[:, j, :])
+            if j == 0:
+                nc.sync.dma_start(offsets[:], offs)
 
-        y = {}
+        woven = {
+            (d, h): keep.tile([P, HALF, PACK], BF16, name="woven%d_%d" % (d, h), align_bytes=64)
+            for d in range(D)
+            for h in range(HALVES)
+        }
 
-        def last_gather():
-            d = D - 1
-            entries = offsets[:, d * V // 16 : (d + 1) * V // 16]
-            nc.scalar.activation(picked[d][:, :, PACK - 1], windows[1][:].indirect(entries), ACT.Copy)
+        def entries(first, count):
+            return offsets[:, first // 16 : (first + count) // 16]
 
-        woven = {}
+        rows = {}
 
-        def weave(d, h, tag=None):
-            rows = slice(h * HALF, (h + 1) * HALF)
-            name = "woven%d_%d" % (d, h)
-            woven[d, h] = keep.tile([P, HALF, PACK], BF16, name=name, tag=tag or name, align_bytes=64)
-            words = pairs[d][:].rearrange("p u n e -> p u (n e)").bitcast(I32)
-            nc.vector.tensor_copy(
-                out=woven[d, h][:].rearrange("p n j -> p (n j)").bitcast(I32).rearrange("p (n u) -> p n u", u=2),
-                in_=words[:, :, rows].rearrange("p u n -> p n u"),
-            )
+        steps = [(d, h) for h in range(HALVES) for d in range(D)]
 
-        def multiply(d, h, tag=None):
-            rows = slice(h * HALF, (h + 1) * HALF)
-            source = woven[d, h][:] if d in WOVEN else picked[d][:, rows, :]
-            name = "codes%d_%d" % (d, h)
-            codes = keep.tile([P, HALF], U32, name=name, tag=tag or name, align_bytes=64)
-            scales = keep.tile([P, HALF], U8, name="scales%d_%d" % (d, h), align_bytes=64)
+        def gather(j, d, h, halves, engine):
+            tile = keep.tile([P, halves * HALF], BF16, name="rows%d_%d_%d" % (j, d, h))
+            looked_up = planes[j][:].indirect(entries(d * V + h * HALF, halves * HALF))
+            if engine is nc.vector:
+                nc.vector.tensor_copy(tile[:], looked_up)
+            else:
+                nc.scalar.activation(tile[:], looked_up, ACT.Copy)
+            for i in range(halves):
+                rows[j, d, h + i] = tile[:, i * HALF : (i + 1) * HALF]
+
+        def weave(j, d, h):
+            nc.vector.tensor_copy(out=woven[d, h][:, :, j], in_=rows[j, d, h])
+
+        def quantize(name, source, width):
+            codes = keep.tile([P, width], U32, name=name + "_codes", align_bytes=64)
+            scales = keep.tile([P, width], U8, name=name + "_scales", align_bytes=64)
             nc.vector.quantize_mx(
-                out=codes[:].bitcast(FP8X4), scales=scales[:], in_=source.rearrange("p n j -> p (n j)")
+                out=codes[:].bitcast(FP8X4), scales=scales[:], in_=source[:].rearrange("p n j -> p (n j)")
             )
-            y[d, h] = psum.tile([P, HALF // P, N], F32, name="y%d_%d" % (d, h), tag="bank%d_%d" % (d, h))
-            for b in range(HALF // P):
-                cols = slice(b * P, (b + 1) * P)
-                nc.tensor.matmul_mx(
-                    out=y[d, h][:, b, :],
-                    lhsT=codes[:, cols].bitcast(FP8X4),
-                    lhsT_scale=scales[:, cols],
-                    rhs=w_codes[:].bitcast(FP8X4),
-                    rhs_scale=w_scales[:],
-                    start=True,
-                    stop=True,
-                )
+            return codes, scales
+
+        for j in range(PACK - 1):
+            gather(j, LAST, 1, 1, nc.vector)
+            weave(j, LAST, 1)
+            for d in range(D):
+                halves = HALVES if d < LAST else 1
+                gather(j, d, 0, halves, nc.scalar)
+                for h in range(halves):
+                    weave(j, d, h)
+
+        packed = {}
+        y = {}
+        copies = {}
+
+        def multiply(b):
+            for half in range(2):
+                y[b, half] = psum.tile([P, 2, N], F32, name="y%d_%d" % (b, half), tag="bank%d_%d" % (b, half))
+                for i in range(2):
+                    d = 2 * half + i
+                    codes, scales = packed[d, b // 2]
+                    first = b % 2 * P
+                    nc.tensor.matmul_mx(
+                        out=y[b, half][:, i, :],
+                        lhsT=codes[:, first : first + P].bitcast(FP8X4),
+                        lhsT_scale=scales[:, first : first + P],
+                        rhs=w_codes[:].bitcast(FP8X4),
+                        rhs_scale=w_scales[:],
+                        start=True,
+                        stop=True,
+                    )
+            copies[b] = keep.tile([P, 2, N], F32, name="copy%d" % b)
+            nc.scalar.copy(out=copies[b][:], in_=y[b, 0][:])
 
         largest = {}
-        copies = {}
-        shifts = {}
+
+        def running_max(b, step):
+            before = copies[b][:, 0, :] if step == 0 else largest[b, step - 1][:]
+            source = (y[b, 1][:, 0, :], y[b, 1][:, 1, :], y[b, 0][:, 1, :])[step]
+            largest[b, step] = keep.tile([P, N], F32, name="largest%d_%d" % (b, step))
+            nc.vector.tensor_tensor(largest[b, step][:], source, before, ALU.max)
+
+        below = {}
         terms = {}
-        totals = {}
-        blocks = [(b, t) for b in range(HALF // P) for t in range(M_TILES)]
+        turned = {}
 
-        def copy_out(d, h):
-            copies[d, h] = keep.tile([P, HALF // P, N], F32, name="copy%d_%d" % (d, h))
-            nc.scalar.copy(out=copies[d, h][:], in_=y[d, h][:])
+        def open_block(b):
+            below[b] = keep.tile([P, D, N], F32, name="below%d" % b, tag="below%d" % b)
+            terms[b] = keep.tile([P, D, N], F32, name="terms%d" % b)
 
-        def running_max(d, h):
-            before = copies[0, h] if d == 1 else largest[d - 1, h]
-            name = "largest%d_%d" % (d, h)
-            largest[d, h] = keep.tile([P, HALF // P, N], F32, name=name, tag=name, align_bytes=64)
-            nc.vector.tensor_tensor(largest[d, h][:], y[d, h][:], before[:], ALU.max)
+        def subtract(b, d0, d1, engine):
+            if engine is nc.gpsimd:
+                source = copies[b][:, d0:d1, :]
+            else:
+                source = y[b, d0 // 2][:, d0 % 2 : d0 % 2 + d1 - d0, :]
+            shift = largest[b, 2][:].unsqueeze(1).to_broadcast([P, d1 - d0, N])
+            engine.tensor_tensor(below[b][:, d0:d1, :], source, shift, ALU.subtract)
 
-        def turn_largest(h):
-            shifts[h] = psum.tile([P, M_TILES, HALF], F32, name="shift%d" % h, tag="bank0_%d" % h)
-            for b, t in blocks:
-                nc.tensor.transpose(
-                    shifts[h][:, t, b * P : (b + 1) * P], largest[D - 1, h][:, b, t * P : (t + 1) * P], identity[:]
-                )
+        def exponential(b, d0, d1):
+            nc.scalar.activation(terms[b][:, d0:d1, :], below[b][:, d0:d1, :], ACT.Exp)
 
-        def exponential(d, h, engine, tag=None):
-            below = keep.tile([P, HALF // P, N], F32, name="below%d_%d" % (d, h), tag="below%d_%d" % (d, h))
-            source = copies[d, h] if (d, h) in copies else y[d, h]
-            engine.tensor_tensor(below[:], source[:], largest[D - 1, h][:], ALU.subtract)
-            name = "term%d_%d" % (d, h)
-            terms[d, h] = keep.tile([P, HALF // P, N], F32, name=name, tag=tag or name)
-            nc.scalar.activation(terms[d, h][:], below[:], ACT.Exp)
+        def turn_largest(b):
+            turned[b] = psum.tile([P, 2, M_TILES, P], F32, name="turned%d" % b, tag="bank%d_0" % b)
+            for t in range(M_TILES):
+                nc.tensor.transpose(turned[b][:, 0, t, :], largest[b, 2][:, t * P : (t + 1) * P], identity[:])
 
-        def add_up(h, order):
-            totals[h] = psum.tile([P, M_TILES, HALF], F32, name="total%d" % h, tag="bank1_%d" % h)
+        def add_up(b, order):
             for i, d in enumerate(order):
-                for b, t in blocks:
+                for t in range(M_TILES):
                     nc.tensor.matmul(
-                        totals[h][:, t, b * P : (b + 1) * P],
-                        terms[d, h][:, b, t * P : (t + 1) * P],
+                        turned[b][:, 1, t, :],
+                        terms[b][:, d, t * P : (t + 1) * P],
                         identity[:],
-                        start=(i == 0 and (b, t) == blocks[0]),
-                        stop=(i == D - 1 and (b, t) == blocks[-1]),
+                        start=(i == 0 and t == 0),
+                        stop=(i == D - 1 and t == M_TILES - 1),
                         is_transpose=True,
                     )
 
-        last_gather()
-        multiply(0, 0)
-        weave(1, 0)
-        multiply(0, 1)
-        multiply(1, 0)
-        weave(2, 0)
-        weave(1, 1)
-        multiply(2, 0)
-        multiply(1, 1)
-        multiply(3, 0)
-        copy_out(0, 0)
-        copy_out(0, 1)
-        running_max(1, 0)
-        copy_out(1, 0)
-        weave(2, 1, "codes3_0")
-        running_max(2, 0)
-        multiply(2, 1)
-        running_max(3, 0)
-        multiply(3, 1, "largest1_0")
-        turn_largest(0)
-        exponential(0, 0, nc.gpsimd)
-        running_max(1, 1)
-        exponential(2, 0, nc.vector)
-        exponential(1, 0, nc.gpsimd, "below2_0")
-        running_max(2, 1)
-        exponential(3, 0, nc.vector)
-        running_max(3, 1)
-        turn_largest(1)
-        add_up(0, (0, 2, 1, 3))
-        exponential(1, 1, nc.vector)
-        exponential(0, 1, nc.vector)
-        exponential(2, 1, nc.vector)
-        exponential(3, 1, nc.vector)
-        add_up(1, (1, 0, 2, 3))
+        j = PACK - 1
+        for i, (d, h) in enumerate(steps):
+            gather(j, d, h, 1, nc.vector if i == 0 else nc.scalar)
+        weave(j, *steps[0])
+        for i, (d, h) in enumerate(steps):
+            if i + 1 < len(steps):
+                weave(j, *steps[i + 1])
+            if i >= len(steps) - 2:
+                running_max(0, i - len(steps) + 2)
+            packed[d, h] = quantize("piece%d_%d" % (d, h), woven[d, h], HALF)
+            if d == LAST:
+                multiply(2 * h)
+                multiply(2 * h + 1)
+        running_max(0, 2)
+        for b in range(BLOCKS - 1):
+            open_block(b)
+            subtract(b, 0, 2, nc.gpsimd)
+            turn_largest(b)
+            running_max(b + 1, 0)
+            subtract(b, 2, 3, nc.vector)
+            running_max(b + 1, 1)
+            subtract(b, 3, 4, nc.vector)
+            running_max(b + 1, 2)
+            exponential(b, 2, 4)
+            exponential(b, 0, 2)
+            add_up(b, (2, 3, 0, 1))
+        b = BLOCKS - 1
+        open_block(b)
+        subtract(b, 0, 1, nc.gpsimd)
+        subtract(b, 2, 4, nc.vector)
+        subtract(b, 1, 2, nc.vector)
+        turn_largest(b)
+        exponential(b, 2, 4)
+        exponential(b, 0, 2)
+        add_up(b, (2, 3, 0, 1))
 
-        for h in range(HALVES):
-            logs = keep.tile([P, M_TILES, HALF], F32, name="logs%d" % h, tag="below%d_%d" % (D - 1 - h, HALVES - 1))
-            for t in range(M_TILES):
-                nc.scalar.activation(logs[:, t, :], totals[h][:, t, :], ACT.Ln)
-                result = keep.tile([P, HALF], F32, name="result%d_%d" % (h, t))
-                nc.vector.tensor_tensor(result[:], shifts[h][:, t, :], logs[:, t, :], ALU.add)
-                nc.sync.dma_start(out=out[t * P : (t + 1) * P, h * HALF : (h + 1) * HALF], in_=result[:])
+        logs = keep.tile([P, BLOCKS, M_TILES, P], F32, name="logs", tag="below%d" % (BLOCKS - 1))
+        out_rows = out.rearrange("(t m) v -> m t v", t=M_TILES)
+        for b in range(BLOCKS):
+            nc.scalar.activation(logs[:, b, :, :], turned[b][:, 1, :, :], ACT.Ln)
+            result = keep.tile([P, M_TILES, P], F32, name="result%d" % b)
+            nc.vector.tensor_tensor(result[:], turned[b][:, 0, :, :], logs[:, b, :, :], ALU.add)
+            nc.sync.dma_start(out=out_rows[:, :, b * P : (b + 1) * P], in_=result[:])

@@ -35,12 +35,12 @@ def tile_picked_lsep_none_e_kernel(tc, xT, w1, offs, out):
         identity = keep.tile([P, P], F32, name="identity")
         make_identity(nc, identity[:])
 
-        w_raw = keep.tile([P, PACK, N], F32, name="w_raw")
         w_grouped = keep.tile([P, N, PACK], BF16, name="w_grouped", align_bytes=64)
         w_codes = keep.tile([P, N], U32, name="w_codes", align_bytes=64)
         w_scales = keep.tile([P, N], U8, name="w_scales", align_bytes=64)
 
         x_rows = xT.rearrange("(p j) t -> p j t", j=PACK)
+        w_raw = keep.tile([P, PACK, N], F32, name="w_raw")
         nc.sync.dma_start(out=w_raw[:], in_=w1.rearrange("(p j) n -> p j n", j=PACK))
         nc.scalar.copy(out=w_grouped[:], in_=w_raw[:].rearrange("p j n -> p n j"))
         nc.vector.quantize_mx(
@@ -54,48 +54,35 @@ def tile_picked_lsep_none_e_kernel(tc, xT, w1, offs, out):
             if j == 0:
                 nc.sync.dma_start(offsets[:], offs)
 
-        woven = {
-            (d, h): keep.tile([P, HALF, PACK], BF16, name="woven%d_%d" % (d, h), align_bytes=64)
-            for d in range(D)
-            for h in range(HALVES)
-        }
+        woven = [keep.tile([P, V, PACK], BF16, name="woven%d" % d, align_bytes=64) for d in range(D)]
 
         def entries(first, count):
             return offsets[:, first // 16 : (first + count) // 16]
 
-        rows = {}
-
-        steps = [(d, h) for h in range(HALVES) for d in range(D)]
-
-        def gather(j, d, h, halves, engine):
-            tile = keep.tile([P, halves * HALF], BF16, name="rows%d_%d_%d" % (j, d, h))
-            looked_up = planes[j][:].indirect(entries(d * V + h * HALF, halves * HALF))
+        def gather(j, first, count, target, engine):
+            looked_up = planes[j][:].indirect(entries(first, count))
             if engine is nc.vector:
-                nc.vector.tensor_copy(tile[:], looked_up)
+                nc.vector.tensor_copy(target, looked_up)
             else:
-                nc.scalar.activation(tile[:], looked_up, ACT.Copy)
-            for i in range(halves):
-                rows[j, d, h + i] = tile[:, i * HALF : (i + 1) * HALF]
+                nc.scalar.activation(target, looked_up, ACT.Copy)
 
-        def weave(j, d, h):
-            nc.vector.tensor_copy(out=woven[d, h][:, :, j], in_=rows[j, d, h])
+        def weave(j, d, first, source):
+            nc.vector.tensor_copy(out=woven[d][:, first : first + source.shape[1], j], in_=source)
 
         def quantize(name, source, width):
             codes = keep.tile([P, width], U32, name=name + "_codes", align_bytes=64)
             scales = keep.tile([P, width], U8, name=name + "_scales", align_bytes=64)
             nc.vector.quantize_mx(
-                out=codes[:].bitcast(FP8X4), scales=scales[:], in_=source[:].rearrange("p n j -> p (n j)")
+                out=codes[:].bitcast(FP8X4), scales=scales[:], in_=source.rearrange("p n j -> p (n j)")
             )
             return codes, scales
 
         for j in range(PACK - 1):
-            gather(j, LAST, 1, 1, nc.vector)
-            weave(j, LAST, 1)
-            for d in range(D):
-                halves = HALVES if d < LAST else 1
-                gather(j, d, 0, halves, nc.scalar)
-                for h in range(halves):
-                    weave(j, d, h)
+            shares = [(LAST, HALF, HALF, nc.vector)] + [(d, 0, V, nc.scalar) for d in range(LAST)]
+            for d, first, count, engine in shares + [(LAST, 0, HALF, nc.scalar)]:
+                rows = keep.tile([P, count], BF16, name="rows%d_%d_%d" % (j, d, first))
+                gather(j, d * V + first, count, rows[:], engine)
+                weave(j, d, first, rows[:])
 
         packed = {}
         y = {}
@@ -125,16 +112,19 @@ def tile_picked_lsep_none_e_kernel(tc, xT, w1, offs, out):
         def running_max(b, step):
             before = copies[b][:, 0, :] if step == 0 else largest[b, step - 1][:]
             source = (y[b, 1][:, 0, :], y[b, 1][:, 1, :], y[b, 0][:, 1, :])[step]
-            largest[b, step] = keep.tile([P, N], F32, name="largest%d_%d" % (b, step))
+            name = "largest%d_%d" % (b, step)
+            largest[b, step] = keep.tile([P, N], F32, name=name, tag=name)
             nc.vector.tensor_tensor(largest[b, step][:], source, before, ALU.max)
 
         below = {}
         terms = {}
         turned = {}
+        totals = {}
 
         def open_block(b):
-            below[b] = keep.tile([P, D, N], F32, name="below%d" % b, tag="below%d" % b)
-            terms[b] = keep.tile([P, D, N], F32, name="terms%d" % b)
+            for half in range(2):
+                name = "below%d_%d" % (b, half)
+                below[b, half] = keep.tile([P, 2, N], F32, name=name, tag=name)
 
         def subtract(b, d0, d1, engine):
             if engine is nc.gpsimd:
@@ -142,22 +132,25 @@ def tile_picked_lsep_none_e_kernel(tc, xT, w1, offs, out):
             else:
                 source = y[b, d0 // 2][:, d0 % 2 : d0 % 2 + d1 - d0, :]
             shift = largest[b, 2][:].unsqueeze(1).to_broadcast([P, d1 - d0, N])
-            engine.tensor_tensor(below[b][:, d0:d1, :], source, shift, ALU.subtract)
+            engine.tensor_tensor(below[b, d0 // 2][:, d0 % 2 : d0 % 2 + d1 - d0, :], source, shift, ALU.subtract)
 
-        def exponential(b, d0, d1):
-            nc.scalar.activation(terms[b][:, d0:d1, :], below[b][:, d0:d1, :], ACT.Exp)
+        def exponential(b, half, tag=None):
+            name = "terms%d_%d" % (b, half)
+            terms[b, half] = keep.tile([P, 2, N], F32, name=name, tag=tag or name)
+            nc.scalar.activation(terms[b, half][:], below[b, half][:], ACT.Exp)
 
         def turn_largest(b):
-            turned[b] = psum.tile([P, 2, M_TILES, P], F32, name="turned%d" % b, tag="bank%d_0" % b)
+            turned[b] = psum.tile([P, M_TILES, P], F32, name="turned%d" % b, tag="bank%d_1" % b)
             for t in range(M_TILES):
-                nc.tensor.transpose(turned[b][:, 0, t, :], largest[b, 2][:, t * P : (t + 1) * P], identity[:])
+                nc.tensor.transpose(turned[b][:, t, :], largest[b, 2][:, t * P : (t + 1) * P], identity[:])
 
         def add_up(b, order):
+            totals[b] = psum.tile([P, M_TILES, P], F32, name="totals%d" % b, tag="bank%d_0" % b)
             for i, d in enumerate(order):
                 for t in range(M_TILES):
                     nc.tensor.matmul(
-                        turned[b][:, 1, t, :],
-                        terms[b][:, d, t * P : (t + 1) * P],
+                        totals[b][:, t, :],
+                        terms[b, d // 2][:, d % 2, t * P : (t + 1) * P],
                         identity[:],
                         start=(i == 0 and t == 0),
                         stop=(i == D - 1 and t == M_TILES - 1),
@@ -165,15 +158,25 @@ def tile_picked_lsep_none_e_kernel(tc, xT, w1, offs, out):
                     )
 
         j = PACK - 1
+        steps = [(d, h) for h in range(HALVES) for d in range(D)]
+        fourth = {}
         for i, (d, h) in enumerate(steps):
-            gather(j, d, h, 1, nc.vector if i == 0 else nc.scalar)
-        weave(j, *steps[0])
+            fourth[d, h] = keep.tile([P, HALF], BF16, name="fourth%d_%d" % (d, h))
+            gather(j, d * V + h * HALF, HALF, fourth[d, h][:], nc.vector if i == 0 else nc.scalar)
+
+        def weave_last(d, h):
+            weave(j, d, h * HALF, fourth[d, h][:])
+
+        weave_last(*steps[0])
         for i, (d, h) in enumerate(steps):
             if i + 1 < len(steps):
-                weave(j, *steps[i + 1])
-            if i >= len(steps) - 2:
-                running_max(0, i - len(steps) + 2)
-            packed[d, h] = quantize("piece%d_%d" % (d, h), woven[d, h], HALF)
+                weave_last(*steps[i + 1])
+            if i == len(steps) - 2:
+                running_max(0, 0)
+            if i == len(steps) - 1:
+                running_max(0, 1)
+                running_max(1, 0)
+            packed[d, h] = quantize("piece%d_%d" % (d, h), woven[d][:, h * HALF : (h + 1) * HALF, :], HALF)
             if d == LAST:
                 multiply(2 * h)
                 multiply(2 * h + 1)
@@ -181,14 +184,14 @@ def tile_picked_lsep_none_e_kernel(tc, xT, w1, offs, out):
         for b in range(BLOCKS - 1):
             open_block(b)
             subtract(b, 0, 2, nc.gpsimd)
-            turn_largest(b)
-            running_max(b + 1, 0)
-            subtract(b, 2, 3, nc.vector)
             running_max(b + 1, 1)
-            subtract(b, 3, 4, nc.vector)
+            subtract(b, 2, 4, nc.vector)
+            turn_largest(b)
+            if b + 2 < BLOCKS:
+                running_max(b + 2, 0)
             running_max(b + 1, 2)
-            exponential(b, 2, 4)
-            exponential(b, 0, 2)
+            exponential(b, 1)
+            exponential(b, 0, "largest%d_1" % (b + 1))
             add_up(b, (2, 3, 0, 1))
         b = BLOCKS - 1
         open_block(b)
@@ -196,14 +199,16 @@ def tile_picked_lsep_none_e_kernel(tc, xT, w1, offs, out):
         subtract(b, 2, 4, nc.vector)
         subtract(b, 1, 2, nc.vector)
         turn_largest(b)
-        exponential(b, 2, 4)
-        exponential(b, 0, 2)
+        exponential(b, 1)
+        exponential(b, 0)
         add_up(b, (2, 3, 0, 1))
 
-        logs = keep.tile([P, BLOCKS, M_TILES, P], F32, name="logs", tag="below%d" % (BLOCKS - 1))
+        logs = keep.tile([P, BLOCKS, M_TILES, P], F32, name="logs", tag="below%d_0" % (BLOCKS - 1))
         out_rows = out.rearrange("(t m) v -> m t v", t=M_TILES)
-        for b in range(BLOCKS):
-            nc.scalar.activation(logs[:, b, :, :], turned[b][:, 1, :, :], ACT.Ln)
-            result = keep.tile([P, M_TILES, P], F32, name="result%d" % b)
-            nc.vector.tensor_tensor(result[:], turned[b][:, 0, :, :], logs[:, b, :, :], ALU.add)
-            nc.sync.dma_start(out=out_rows[:, :, b * P : (b + 1) * P], in_=result[:])
+        steps = [(b, slice(0, M_TILES)) for b in range(BLOCKS - 1)]
+        steps.extend((BLOCKS - 1, slice(t, t + 1)) for t in range(M_TILES))
+        for b, tiles in steps:
+            nc.scalar.activation(logs[:, b, tiles, :], totals[b][:, tiles, :], ACT.Ln)
+            result = keep.tile([P, tiles.stop - tiles.start, P], F32, name="result%d_%d" % (b, tiles.start))
+            nc.vector.tensor_tensor(result[:], turned[b][:, tiles, :], logs[:, b, tiles, :], ALU.add)
+            nc.sync.dma_start(out=out_rows[:, tiles, b * P : (b + 1) * P], in_=result[:])

@@ -162,12 +162,16 @@ def tile_picked_lsep_none_e_kernel(tc, xT, w1, offs, out):
         fourth = {}
         for i, (d, h) in enumerate(steps):
             fourth[d, h] = keep.tile([P, HALF], BF16, name="fourth%d_%d" % (d, h))
-            gather(j, d * V + h * HALF, HALF, fourth[d, h][:], nc.vector if i == 0 else nc.scalar)
+            parts = 2 if i == 0 else 1
+            for part in range(parts):
+                cols = slice(part * HALF // parts, (part + 1) * HALF // parts)
+                gather(j, d * V + h * HALF + cols.start, HALF // parts, fourth[d, h][:, cols], nc.scalar)
 
         def weave_last(d, h):
             weave(j, d, h * HALF, fourth[d, h][:])
 
-        weave_last(*steps[0])
+        for part in range(2):
+            weave(j, 0, part * P, fourth[0, 0][:, part * P : (part + 1) * P])
         for i, (d, h) in enumerate(steps):
             if i + 1 < len(steps):
                 weave_last(*steps[i + 1])
@@ -176,11 +180,11 @@ def tile_picked_lsep_none_e_kernel(tc, xT, w1, offs, out):
             if i == len(steps) - 1:
                 running_max(0, 1)
                 running_max(1, 0)
+                running_max(0, 2)
             packed[d, h] = quantize("piece%d_%d" % (d, h), woven[d][:, h * HALF : (h + 1) * HALF, :], HALF)
             if d == LAST:
                 multiply(2 * h)
                 multiply(2 * h + 1)
-        running_max(0, 2)
         for b in range(BLOCKS - 1):
             open_block(b)
             subtract(b, 0, 2, nc.gpsimd)
@@ -195,9 +199,8 @@ def tile_picked_lsep_none_e_kernel(tc, xT, w1, offs, out):
             add_up(b, (2, 3, 0, 1))
         b = BLOCKS - 1
         open_block(b)
-        subtract(b, 0, 1, nc.gpsimd)
         subtract(b, 2, 4, nc.vector)
-        subtract(b, 1, 2, nc.vector)
+        subtract(b, 0, 2, nc.vector)
         turn_largest(b)
         exponential(b, 1)
         exponential(b, 0)

@@ -140,20 +140,22 @@ def tile_picked_lsep_none_e_kernel(tc, xT, w1, offs, out):
             nc.scalar.activation(terms[b, half][:], below[b, half][:], ACT.Exp)
 
         def turn_largest(b):
-            turned[b] = psum.tile([P, M_TILES, P], F32, name="turned%d" % b, tag="bank%d_1" % b)
             for t in range(M_TILES):
-                nc.tensor.transpose(turned[b][:, t, :], largest[b, 2][:, t * P : (t + 1) * P], identity[:])
+                if b == 0:
+                    turned[t] = psum.tile([P, V], F32, name="turned%d" % t, tag="bank%d_1" % t)
+                nc.tensor.transpose(turned[t][:, b * P : (b + 1) * P], largest[b, 2][:, t * P : (t + 1) * P], identity[:])
 
         def add_up(b, order):
-            totals[b] = psum.tile([P, M_TILES, P], F32, name="totals%d" % b, tag="bank%d_0" % b)
             for i, d in enumerate(order):
                 for t in range(M_TILES):
+                    if b == 0 and i == 0:
+                        totals[t] = psum.tile([P, V], F32, name="totals%d" % t, tag="bank%d_0" % t)
                     nc.tensor.matmul(
-                        totals[b][:, t, :],
+                        totals[t][:, b * P : (b + 1) * P],
                         terms[b, d // 2][:, d % 2, t * P : (t + 1) * P],
                         identity[:],
-                        start=(i == 0 and t == 0),
-                        stop=(i == D - 1 and t == M_TILES - 1),
+                        start=(i == 0),
+                        stop=(i == D - 1),
                         is_transpose=True,
                     )
 
@@ -188,15 +190,17 @@ def tile_picked_lsep_none_e_kernel(tc, xT, w1, offs, out):
         for b in range(BLOCKS - 1):
             open_block(b)
             subtract(b, 0, 2, nc.gpsimd)
-            running_max(b + 1, 1)
-            subtract(b, 2, 4, nc.vector)
-            turn_largest(b)
             if b + 2 < BLOCKS:
                 running_max(b + 2, 0)
+            running_max(b + 1, 1)
+            subtract(b, 2, 4, nc.vector)
+            if b > 0:
+                turn_largest(b - 1)
             running_max(b + 1, 2)
             exponential(b, 1)
             exponential(b, 0, "largest%d_1" % (b + 1))
             add_up(b, (2, 3, 0, 1))
+        turn_largest(BLOCKS - 2)
         b = BLOCKS - 1
         open_block(b)
         subtract(b, 2, 4, nc.vector)
@@ -206,12 +210,11 @@ def tile_picked_lsep_none_e_kernel(tc, xT, w1, offs, out):
         exponential(b, 0)
         add_up(b, (2, 3, 0, 1))
 
-        logs = keep.tile([P, BLOCKS, M_TILES, P], F32, name="logs", tag="below%d_0" % (BLOCKS - 1))
-        out_rows = out.rearrange("(t m) v -> m t v", t=M_TILES)
-        steps = [(b, slice(0, M_TILES)) for b in range(BLOCKS - 1)]
-        steps.extend((BLOCKS - 1, slice(t, t + 1)) for t in range(M_TILES))
-        for b, tiles in steps:
-            nc.scalar.activation(logs[:, b, tiles, :], totals[b][:, tiles, :], ACT.Ln)
-            result = keep.tile([P, tiles.stop - tiles.start, P], F32, name="result%d_%d" % (b, tiles.start))
-            nc.vector.tensor_tensor(result[:], turned[b][:, tiles, :], logs[:, b, tiles, :], ALU.add)
-            nc.sync.dma_start(out=out_rows[:, tiles, b * P : (b + 1) * P], in_=result[:])
+        logs = keep.tile([P, M_TILES, V], F32, name="logs", tag="below%d_0" % (BLOCKS - 1))
+        for t in range(M_TILES):
+            for h in range(HALVES):
+                places = slice(h * HALF, (h + 1) * HALF)
+                nc.scalar.activation(logs[:, t, places], totals[t][:, places], ACT.Ln)
+                result = keep.tile([P, HALF], F32, name="result%d_%d" % (t, h))
+                nc.vector.tensor_tensor(result[:], turned[t][:, places], logs[:, t, places], ALU.add)
+                nc.sync.dma_start(out=out[t * P : (t + 1) * P, places], in_=result[:])

@@ -104,8 +104,9 @@ def tile_picked_lsep_none_e_kernel(tc, xT, w1, offs, out):
                         start=True,
                         stop=True,
                     )
-            copies[b] = keep.tile([P, 2, N], F32, name="copy%d" % b)
-            nc.scalar.copy(out=copies[b][:], in_=y[b, 0][:])
+            kept = 2 if b + 1 < BLOCKS else 1
+            copies[b] = keep.tile([P, kept, N], F32, name="copy%d" % b)
+            nc.scalar.copy(out=copies[b][:], in_=y[b, 0][:, 0:kept, :])
 
         largest = {}
 
@@ -162,31 +163,46 @@ def tile_picked_lsep_none_e_kernel(tc, xT, w1, offs, out):
         j = PACK - 1
         steps = [(d, h) for h in range(HALVES) for d in range(D)]
         fourth = {}
-        for i, (d, h) in enumerate(steps):
-            fourth[d, h] = keep.tile([P, HALF], BF16, name="fourth%d_%d" % (d, h))
-            parts = 2 if i == 0 else 1
-            for part in range(parts):
-                cols = slice(part * HALF // parts, (part + 1) * HALF // parts)
-                gather(j, d * V + h * HALF + cols.start, HALF // parts, fourth[d, h][:, cols], nc.scalar)
 
-        def weave_last(d, h):
-            weave(j, d, h * HALF, fourth[d, h][:])
+        def gather_last(i, cols, engine, tag=None):
+            d, h = steps[i]
+            if i not in fourth:
+                name = "fourth%d" % i
+                fourth[i] = keep.tile([P, HALF], BF16, name=name, tag=tag or name)
+            gather(j, d * V + h * HALF + cols.start, cols.stop - cols.start, fourth[i][:, cols], engine)
 
-        for part in range(2):
-            weave(j, 0, part * P, fourth[0, 0][:, part * P : (part + 1) * P])
-        for i, (d, h) in enumerate(steps):
-            if i + 1 < len(steps):
-                weave_last(*steps[i + 1])
-            if i == len(steps) - 2:
-                running_max(0, 0)
-            if i == len(steps) - 1:
-                running_max(0, 1)
-                running_max(1, 0)
-                running_max(0, 2)
+        def weave_last(i, cols):
+            d, h = steps[i]
+            weave(j, d, h * HALF + cols.start, fourth[i][:, cols])
+
+        def quantize_step(i):
+            d, h = steps[i]
             packed[d, h] = quantize("piece%d_%d" % (d, h), woven[d][:, h * HALF : (h + 1) * HALF, :], HALF)
-            if d == LAST:
-                multiply(2 * h)
-                multiply(2 * h + 1)
+
+        whole = slice(0, HALF)
+        final = len(steps) - 1
+        gather_last(0, slice(0, P), nc.vector)
+        gather_last(0, slice(P, HALF), nc.scalar)
+        for i in range(1, final):
+            gather_last(i, whole, nc.scalar)
+        weave_last(0, slice(0, P))
+        weave_last(0, slice(P, HALF))
+        for i in range(final - 1):
+            weave_last(i + 1, whole)
+            quantize_step(i)
+            if i == LAST:
+                multiply(0)
+                multiply(1)
+        gather_last(final, whole, nc.scalar, "fourth%d" % (final - 2))
+        nc.scalar.copy(out=woven[LAST][:, HALF:V, j], in_=fourth[final][:])
+        running_max(0, 0)
+        quantize_step(final - 1)
+        running_max(0, 1)
+        running_max(1, 0)
+        running_max(0, 2)
+        quantize_step(final)
+        multiply(2)
+        multiply(3)
         for b in range(BLOCKS - 1):
             open_block(b)
             subtract(b, 0, 2, nc.gpsimd)
@@ -203,8 +219,9 @@ def tile_picked_lsep_none_e_kernel(tc, xT, w1, offs, out):
         turn_largest(BLOCKS - 2)
         b = BLOCKS - 1
         open_block(b)
+        subtract(b, 0, 1, nc.gpsimd)
         subtract(b, 2, 4, nc.vector)
-        subtract(b, 0, 2, nc.vector)
+        subtract(b, 1, 2, nc.vector)
         turn_largest(b)
         exponential(b, 1)
         exponential(b, 0)

@@ -22,6 +22,7 @@ M_TILES = N // P
 BLOCKS = V // P
 LAST = D - 1
 HALVES = 2
+SCALAR_REST = 192
 HALF = V // HALVES
 
 
@@ -78,8 +79,9 @@ def tile_picked_lsep_none_e_kernel(tc, xT, w1, offs, out):
             return codes, scales
 
         for j in range(PACK - 1):
-            shares = [(LAST, HALF, HALF, nc.vector)] + [(d, 0, V, nc.scalar) for d in range(LAST)]
-            for d, first, count, engine in shares + [(LAST, 0, HALF, nc.scalar)]:
+            shares = [(LAST, SCALAR_REST, V - SCALAR_REST, nc.vector)] + [(d, 0, V, nc.scalar) for d in range(LAST - 1)]
+            shares.extend((LAST - 1, h * HALF, HALF, nc.scalar) for h in range(HALVES))
+            for d, first, count, engine in shares + [(LAST, 0, SCALAR_REST, nc.scalar)]:
                 rows = keep.tile([P, count], BF16, name="rows%d_%d_%d" % (j, d, first))
                 gather(j, d * V + first, count, rows[:], engine)
                 weave(j, d, first, rows[:])

@@ -22,7 +22,7 @@ M_TILES = N // P
 BLOCKS = V // P
 LAST = D - 1
 HALVES = 2
-SCALAR_REST = 192
+EARLY_VECTOR = (1024, 768)
 HALF = V // HALVES
 
 
@@ -67,9 +67,6 @@ def tile_picked_lsep_none_e_kernel(tc, xT, w1, offs, out):
             else:
                 nc.scalar.activation(target, looked_up, ACT.Copy)
 
-        def weave(j, d, first, source):
-            nc.vector.tensor_copy(out=woven[d][:, first : first + source.shape[1], j], in_=source)
-
         def quantize(name, source, width):
             codes = keep.tile([P, width], U32, name=name + "_codes", align_bytes=64)
             scales = keep.tile([P, width], U8, name=name + "_scales", align_bytes=64)
@@ -78,13 +75,19 @@ def tile_picked_lsep_none_e_kernel(tc, xT, w1, offs, out):
             )
             return codes, scales
 
-        for j in range(PACK - 1):
-            shares = [(LAST, SCALAR_REST, V - SCALAR_REST, nc.vector)] + [(d, 0, V, nc.scalar) for d in range(LAST - 1)]
-            shares.extend((LAST - 1, h * HALF, HALF, nc.scalar) for h in range(HALVES))
-            for d, first, count, engine in shares + [(LAST, 0, SCALAR_REST, nc.scalar)]:
-                rows = keep.tile([P, count], BF16, name="rows%d_%d_%d" % (j, d, first))
-                gather(j, d * V + first, count, rows[:], engine)
-                weave(j, d, first, rows[:])
+        early = keep.tile([P, 2, S], BF16, name="early")
+        for j in range(2):
+            split = EARLY_VECTOR[j]
+            gather(j, 0, split, early[:, j, 0:split], nc.vector)
+            gather(j, split, S - split, early[:, j, split:S], nc.scalar)
+        for d in range(D):
+            nc.vector.tensor_copy(
+                out=woven[d][:, :, 0:2], in_=early[:, :, d * V : (d + 1) * V].rearrange("p j n -> p n j")
+            )
+        steps = [(d, h) for h in range(HALVES) for d in range(D)]
+        late = [keep.tile([P, 2, HALF], BF16, name="late%d" % i) for i in range(len(steps))]
+        for i, (d, h) in enumerate(steps):
+            gather(2, d * V + h * HALF, HALF, late[i][:, 0, :], nc.vector if i % 4 == 0 else nc.scalar)
 
         packed = {}
         y = {}
@@ -162,20 +165,14 @@ def tile_picked_lsep_none_e_kernel(tc, xT, w1, offs, out):
                         is_transpose=True,
                     )
 
-        j = PACK - 1
-        steps = [(d, h) for h in range(HALVES) for d in range(D)]
-        fourth = {}
-
-        def gather_last(i, cols, engine, tag=None):
+        def gather_last(i, cols, engine):
             d, h = steps[i]
-            if i not in fourth:
-                name = "fourth%d" % i
-                fourth[i] = keep.tile([P, HALF], BF16, name=name, tag=tag or name)
-            gather(j, d * V + h * HALF + cols.start, cols.stop - cols.start, fourth[i][:, cols], engine)
+            gather(3, d * V + h * HALF + cols.start, cols.stop - cols.start, late[i][:, 1, cols], engine)
 
-        def weave_last(i, cols):
+        def weave_last(i, cols, copy=nc.vector.tensor_copy):
             d, h = steps[i]
-            weave(j, d, h * HALF + cols.start, fourth[i][:, cols])
+            places = slice(h * HALF + cols.start, h * HALF + cols.stop)
+            copy(out=woven[d][:, places, 2:4], in_=late[i][:, :, cols].rearrange("p j n -> p n j"))
 
         def quantize_step(i):
             d, h = steps[i]
@@ -195,8 +192,8 @@ def tile_picked_lsep_none_e_kernel(tc, xT, w1, offs, out):
             if i == LAST:
                 multiply(0)
                 multiply(1)
-        gather_last(final, whole, nc.scalar, "fourth%d" % (final - 2))
-        nc.scalar.copy(out=woven[LAST][:, HALF:V, j], in_=fourth[final][:])
+        gather_last(final, whole, nc.scalar)
+        weave_last(final, whole, nc.scalar.copy)
         running_max(0, 0)
         quantize_step(final - 1)
         running_max(0, 1)

@@ -1,5 +1,7 @@
 from contextlib import ExitStack
 
+import math
+
 import concourse.mybir as mybir
 from concourse.masks import make_identity
 
@@ -24,6 +26,7 @@ LAST = D - 1
 HALVES = 2
 EARLY_VECTOR = (1024, 768)
 HALF = V // HALVES
+CAP = 30.0
 
 
 def tile_picked_lsep_none_e_kernel(tc, xT, w1, offs, out):
@@ -117,7 +120,7 @@ def tile_picked_lsep_none_e_kernel(tc, xT, w1, offs, out):
 
         def running_max(b, step):
             before = copies[b][:, 0, :] if step == 0 else largest[b, step - 1][:]
-            source = (y[b, 1][:, 0, :], y[b, 1][:, 1, :], y[b, 0][:, 1, :])[step]
+            source = (y[b, 1][:, 0, :], y[b, 0][:, 1, :])[step]
             name = "largest%d_%d" % (b, step)
             largest[b, step] = keep.tile([P, N], F32, name=name, tag=name)
             nc.vector.tensor_tensor(largest[b, step][:], source, before, ALU.max)
@@ -137,19 +140,13 @@ def tile_picked_lsep_none_e_kernel(tc, xT, w1, offs, out):
                 source = copies[b][:, d0:d1, :]
             else:
                 source = y[b, d0 // 2][:, d0 % 2 : d0 % 2 + d1 - d0, :]
-            shift = largest[b, 2][:].unsqueeze(1).to_broadcast([P, d1 - d0, N])
+            shift = largest[b, 1][:].unsqueeze(1).to_broadcast([P, d1 - d0, N])
             engine.tensor_tensor(below[b, d0 // 2][:, d0 % 2 : d0 % 2 + d1 - d0, :], source, shift, ALU.subtract)
 
         def exponential(b, half, tag=None):
             name = "terms%d_%d" % (b, half)
             terms[b, half] = keep.tile([P, 2, N], F32, name=name, tag=tag or name)
             nc.scalar.activation(terms[b, half][:], below[b, half][:], ACT.Exp)
-
-        def turn_largest(b):
-            for t in range(M_TILES):
-                if b == 0:
-                    turned[t] = psum.tile([P, V], F32, name="turned%d" % t, tag="bank%d_1" % t)
-                nc.tensor.transpose(turned[t][:, b * P : (b + 1) * P], largest[b, 2][:, t * P : (t + 1) * P], identity[:])
 
         def add_up(b, order):
             for i, d in enumerate(order):
@@ -196,41 +193,48 @@ def tile_picked_lsep_none_e_kernel(tc, xT, w1, offs, out):
         weave_last(final, whole, nc.scalar.copy)
         running_max(0, 0)
         quantize_step(final - 1)
-        running_max(0, 1)
         running_max(1, 0)
-        running_max(0, 2)
+        running_max(0, 1)
         quantize_step(final)
         multiply(2)
         multiply(3)
         for b in range(BLOCKS - 1):
             open_block(b)
             subtract(b, 0, 2, nc.gpsimd)
+            subtract(b, 2, 4, nc.vector)
+            running_max(b + 1, 1)
             if b + 2 < BLOCKS:
                 running_max(b + 2, 0)
-            running_max(b + 1, 1)
-            subtract(b, 2, 4, nc.vector)
-            if b > 0:
-                turn_largest(b - 1)
-            running_max(b + 1, 2)
             exponential(b, 1)
-            exponential(b, 0, "largest%d_1" % (b + 1))
+            exponential(b, 0, "largest%d_0" % (b + 1))
             add_up(b, (2, 3, 0, 1))
-        turn_largest(BLOCKS - 2)
         b = BLOCKS - 1
         open_block(b)
         subtract(b, 0, 1, nc.gpsimd)
         subtract(b, 2, 4, nc.vector)
         subtract(b, 1, 2, nc.vector)
-        turn_largest(b)
         exponential(b, 1)
         exponential(b, 0)
         add_up(b, (2, 3, 0, 1))
+
+        shifts = keep.tile([P, BLOCKS, N], F32, name="shifts", tag="copy%d" % (BLOCKS - 1))
+        for b in range(BLOCKS):
+            nc.vector.scalar_tensor_tensor(
+                out=shifts[:, b, :], in0=y[b, 1][:, 1, :], scalar=-CAP, in1=largest[b, 1][:], op0=ALU.add, op1=ALU.max
+            )
+        capped = {}
+        for t in range(M_TILES):
+            capped[t] = keep.tile([P, V], F32, name="capped%d" % t)
+            nc.vector.tensor_scalar_min(capped[t][:], totals[t][:], math.exp(CAP))
+            turned[t] = psum.tile([P, V], F32, name="turned%d" % t, tag="bank%d_0" % (2 + t))
+            for b in range(BLOCKS):
+                nc.tensor.transpose(turned[t][:, b * P : (b + 1) * P], shifts[:, b, t * P : (t + 1) * P], identity[:])
 
         logs = keep.tile([P, M_TILES, V], F32, name="logs", tag="below%d_0" % (BLOCKS - 1))
         for t in range(M_TILES):
             for h in range(HALVES):
                 places = slice(h * HALF, (h + 1) * HALF)
-                nc.scalar.activation(logs[:, t, places], totals[t][:, places], ACT.Ln)
+                nc.scalar.activation(logs[:, t, places], capped[t][:, places], ACT.Ln)
                 result = keep.tile([P, HALF], F32, name="result%d_%d" % (t, h))
                 nc.vector.tensor_tensor(result[:], turned[t][:, places], logs[:, t, places], ALU.add)
                 nc.sync.dma_start(out=out[t * P : (t + 1) * P, places], in_=result[:])

@@ -24,7 +24,7 @@ M_TILES = N // P
 BLOCKS = V // P
 LAST = D - 1
 HALVES = 2
-EARLY_VECTOR = (1024, 768)
+PAIRED = (5, 6)
 HALF = V // HALVES
 CAP = 30.0
 
@@ -78,19 +78,24 @@ def tile_picked_lsep_none_e_kernel(tc, xT, w1, offs, out):
             )
             return codes, scales
 
-        early = keep.tile([P, 2, S], BF16, name="early")
         for j in range(2):
-            split = EARLY_VECTOR[j]
-            gather(j, 0, split, early[:, j, 0:split], nc.vector)
-            gather(j, split, S - split, early[:, j, split:S], nc.scalar)
-        for d in range(D):
-            nc.vector.tensor_copy(
-                out=woven[d][:, :, 0:2], in_=early[:, :, d * V : (d + 1) * V].rearrange("p j n -> p n j")
-            )
+            rows = keep.tile([P, S], BF16, name="rows%d" % j)
+            gather(j, 0, HALF, rows[:, 0:HALF], nc.vector)
+            first = HALF
+            for last in (V, 2 * V, 3 * V, S - HALF, S):
+                gather(j, first, last - first, rows[:, first:last], nc.scalar)
+                d = first // V
+                begin = d * V if last < S else first
+                nc.vector.tensor_copy(out=woven[d][:, begin - d * V : last - d * V, j], in_=rows[:, begin:last])
+                first = last
         steps = [(d, h) for h in range(HALVES) for d in range(D)]
+        final = len(steps) - 1
         late = [keep.tile([P, 2, HALF], BF16, name="late%d" % i) for i in range(len(steps))]
-        for i, (d, h) in enumerate(steps):
-            gather(2, d * V + h * HALF, HALF, late[i][:, 0, :], nc.vector if i % 4 == 0 else nc.scalar)
+        for i in [0, final] + list(range(1, final)):
+            d, h = steps[i]
+            gather(2, d * V + h * HALF, HALF, late[i][:, 0, :], nc.vector if i in (0, final - 1) else nc.scalar)
+            if i not in PAIRED:
+                nc.vector.tensor_copy(out=woven[d][:, h * HALF : (h + 1) * HALF, 2], in_=late[i][:, 0, :])
 
         packed = {}
         y = {}
@@ -149,16 +154,17 @@ def tile_picked_lsep_none_e_kernel(tc, xT, w1, offs, out):
             nc.scalar.activation(terms[b, half][:], below[b, half][:], ACT.Exp)
 
         def add_up(b, order):
+            h = b // 2
             for i, d in enumerate(order):
                 for t in range(M_TILES):
-                    if b == 0 and i == 0:
-                        totals[t] = psum.tile([P, V], F32, name="totals%d" % t, tag="bank%d_0" % t)
+                    if b % 2 == 0 and i == 0 and t == 0:
+                        totals[h] = psum.tile([P, M_TILES, HALF], F32, name="totals%d" % h, tag="bank%d_0" % (2 * h))
                     nc.tensor.matmul(
-                        totals[t][:, b * P : (b + 1) * P],
+                        totals[h][:, t, b % 2 * P : (b % 2 + 1) * P],
                         terms[b, d // 2][:, d % 2, t * P : (t + 1) * P],
                         identity[:],
-                        start=(i == 0),
-                        stop=(i == D - 1),
+                        start=(i == 0 and t == 0),
+                        stop=(i == D - 1 and t == M_TILES - 1),
                         is_transpose=True,
                     )
 
@@ -169,14 +175,16 @@ def tile_picked_lsep_none_e_kernel(tc, xT, w1, offs, out):
         def weave_last(i, cols, copy=nc.vector.tensor_copy):
             d, h = steps[i]
             places = slice(h * HALF + cols.start, h * HALF + cols.stop)
-            copy(out=woven[d][:, places, 2:4], in_=late[i][:, :, cols].rearrange("p j n -> p n j"))
+            if i in PAIRED:
+                copy(out=woven[d][:, places, 2:4], in_=late[i][:, :, cols].rearrange("p j n -> p n j"))
+            else:
+                copy(out=woven[d][:, places, 3], in_=late[i][:, 1, cols])
 
         def quantize_step(i):
             d, h = steps[i]
             packed[d, h] = quantize("piece%d_%d" % (d, h), woven[d][:, h * HALF : (h + 1) * HALF, :], HALF)
 
         whole = slice(0, HALF)
-        final = len(steps) - 1
         gather_last(0, slice(0, P), nc.vector)
         gather_last(0, slice(P, HALF), nc.scalar)
         for i in range(1, final):
@@ -217,24 +225,32 @@ def tile_picked_lsep_none_e_kernel(tc, xT, w1, offs, out):
         exponential(b, 0)
         add_up(b, (2, 3, 0, 1))
 
+        capped = {}
+
+        def cap(h, tag):
+            capped[h] = keep.tile([P, M_TILES, HALF], F32, name="capped%d" % h, tag=tag)
+            nc.vector.tensor_scalar_min(capped[h][:], totals[h][:], math.exp(CAP))
+
+        cap(0, "below%d_0" % (BLOCKS - 1))
         shifts = keep.tile([P, BLOCKS, N], F32, name="shifts", tag="copy%d" % (BLOCKS - 1))
         for b in range(BLOCKS):
             nc.vector.scalar_tensor_tensor(
                 out=shifts[:, b, :], in0=y[b, 1][:, 1, :], scalar=-CAP, in1=largest[b, 1][:], op0=ALU.add, op1=ALU.max
             )
-        capped = {}
-        for t in range(M_TILES):
-            capped[t] = keep.tile([P, V], F32, name="capped%d" % t)
-            nc.vector.tensor_scalar_min(capped[t][:], totals[t][:], math.exp(CAP))
-            turned[t] = psum.tile([P, V], F32, name="turned%d" % t, tag="bank%d_0" % (2 + t))
-            for b in range(BLOCKS):
-                nc.tensor.transpose(turned[t][:, b * P : (b + 1) * P], shifts[:, b, t * P : (t + 1) * P], identity[:])
+        cap(1, "capped1")
+        for h in range(HALVES):
+            turned[h] = psum.tile([P, M_TILES, HALF], F32, name="turned%d" % h, tag="bank%d_1" % (2 + h))
+            for t in range(M_TILES):
+                for b in range(2 * h, 2 * h + 2):
+                    nc.tensor.transpose(
+                        turned[h][:, t, b % 2 * P : (b % 2 + 1) * P], shifts[:, b, t * P : (t + 1) * P], identity[:]
+                    )
 
-        logs = keep.tile([P, M_TILES, V], F32, name="logs", tag="below%d_0" % (BLOCKS - 1))
-        for t in range(M_TILES):
-            for h in range(HALVES):
+        logs = keep.tile([P, M_TILES, V], F32, name="logs")
+        for h in range(HALVES):
+            for t in range(M_TILES):
                 places = slice(h * HALF, (h + 1) * HALF)
-                nc.scalar.activation(logs[:, t, places], capped[t][:, places], ACT.Ln)
+                nc.scalar.activation(logs[:, t, places], capped[h][:, t, :], ACT.Ln)
                 result = keep.tile([P, HALF], F32, name="result%d_%d" % (t, h))
-                nc.vector.tensor_tensor(result[:], turned[t][:, places], logs[:, t, places], ALU.add)
+                nc.vector.tensor_tensor(result[:], turned[h][:, t, :], logs[:, t, places], ALU.add)
                 nc.sync.dma_start(out=out[t * P : (t + 1) * P, places], in_=result[:])

@@ -117,7 +117,7 @@ def tile_picked_lsep_none_e_kernel(tc, xT, w1, offs, out):
                         start=True,
                         stop=True,
                     )
-            kept = 2 if b + 1 < BLOCKS else 1
+            kept = 2 if b < 2 else 1
             copies[b] = keep.tile([P, kept, N], F32, name="copy%d" % b)
             nc.scalar.copy(out=copies[b][:], in_=y[b, 0][:, 0:kept, :])
 
@@ -153,20 +153,35 @@ def tile_picked_lsep_none_e_kernel(tc, xT, w1, offs, out):
             terms[b, half] = keep.tile([P, 2, N], F32, name=name, tag=tag or name)
             nc.scalar.activation(terms[b, half][:], below[b, half][:], ACT.Exp)
 
-        def add_up(b, order):
+        def add_up(b, addends, opens, closes):
             h = b // 2
-            for i, d in enumerate(order):
+            for i, addend in enumerate(addends):
                 for t in range(M_TILES):
-                    if b % 2 == 0 and i == 0 and t == 0:
+                    if h not in totals:
                         totals[h] = psum.tile([P, M_TILES, HALF], F32, name="totals%d" % h, tag="bank%d_0" % (2 * h))
                     nc.tensor.matmul(
                         totals[h][:, t, b % 2 * P : (b % 2 + 1) * P],
-                        terms[b, d // 2][:, d % 2, t * P : (t + 1) * P],
+                        addend[:, t * P : (t + 1) * P],
                         identity[:],
-                        start=(i == 0 and t == 0),
-                        stop=(i == D - 1 and t == M_TILES - 1),
+                        start=(opens and i == 0 and t == 0),
+                        stop=(closes and i == len(addends) - 1 and t == M_TILES - 1),
                         is_transpose=True,
                     )
+
+        def pair(b, half):
+            return [terms[b, half][:, 0, :], terms[b, half][:, 1, :]]
+
+        def join(b):
+            joined = keep.tile([P, N], F32, name="joined%d" % b)
+            nc.vector.scalar_tensor_tensor(
+                out=joined[:],
+                in0=terms[b, 1][:, 1, :],
+                scalar=math.exp(CAP),
+                in1=terms[b, 1][:, 0, :],
+                op0=ALU.min,
+                op1=ALU.add,
+            )
+            return [joined[:]]
 
         def gather_last(i, cols, engine):
             d, h = steps[i]
@@ -208,14 +223,19 @@ def tile_picked_lsep_none_e_kernel(tc, xT, w1, offs, out):
         multiply(3)
         for b in range(BLOCKS - 1):
             open_block(b)
-            subtract(b, 0, 2, nc.gpsimd)
+            subtract(b, 0, 2 if b < 2 else 1, nc.gpsimd)
             subtract(b, 2, 4, nc.vector)
             running_max(b + 1, 1)
+            if b == 2:
+                subtract(b, 1, 2, nc.vector)
             if b + 2 < BLOCKS:
                 running_max(b + 2, 0)
             exponential(b, 1)
             exponential(b, 0, "largest%d_0" % (b + 1))
-            add_up(b, (2, 3, 0, 1))
+            if b < 2:
+                add_up(b, pair(b, 1) + pair(b, 0), True, True)
+            else:
+                add_up(b, pair(b, 0), True, False)
         b = BLOCKS - 1
         open_block(b)
         subtract(b, 0, 1, nc.gpsimd)
@@ -223,25 +243,20 @@ def tile_picked_lsep_none_e_kernel(tc, xT, w1, offs, out):
         subtract(b, 1, 2, nc.vector)
         exponential(b, 1)
         exponential(b, 0)
-        add_up(b, (2, 3, 0, 1))
+        add_up(b - 1, join(b - 1), False, False)
+        add_up(b, join(b) + pair(b, 0), False, True)
 
-        capped = {}
-
-        def cap(h, tag):
-            capped[h] = keep.tile([P, M_TILES, HALF], F32, name="capped%d" % h, tag=tag)
-            nc.vector.tensor_scalar_min(capped[h][:], totals[h][:], math.exp(CAP))
-
-        cap(0, "below%d_0" % (BLOCKS - 1))
         shifts = keep.tile([P, BLOCKS, N], F32, name="shifts", tag="copy%d" % (BLOCKS - 1))
         for b in range(BLOCKS):
             nc.vector.scalar_tensor_tensor(
                 out=shifts[:, b, :], in0=y[b, 1][:, 1, :], scalar=-CAP, in1=largest[b, 1][:], op0=ALU.add, op1=ALU.max
             )
-        cap(1, "capped1")
+        capped = keep.tile([P, M_TILES, HALF], F32, name="capped", tag="below%d_0" % (BLOCKS - 1))
+        nc.vector.tensor_scalar_min(capped[:], totals[0][:], math.exp(CAP))
         for h in range(HALVES):
-            turned[h] = psum.tile([P, M_TILES, HALF], F32, name="turned%d" % h, tag="bank%d_1" % (2 + h))
-            for t in range(M_TILES):
-                for b in range(2 * h, 2 * h + 2):
+            turned[h] = psum.tile([P, M_TILES, HALF], F32, name="turned%d" % h, tag="bank%d_0" % (2 * h + 1))
+            for b in range(2 * h, 2 * h + 2):
+                for t in range(M_TILES):
                     nc.tensor.transpose(
                         turned[h][:, t, b % 2 * P : (b % 2 + 1) * P], shifts[:, b, t * P : (t + 1) * P], identity[:]
                     )
@@ -250,7 +265,7 @@ def tile_picked_lsep_none_e_kernel(tc, xT, w1, offs, out):
         for h in range(HALVES):
             for t in range(M_TILES):
                 places = slice(h * HALF, (h + 1) * HALF)
-                nc.scalar.activation(logs[:, t, places], capped[h][:, t, :], ACT.Ln)
+                nc.scalar.activation(logs[:, t, places], (capped, totals[1])[h][:, t, :], ACT.Ln)
                 result = keep.tile([P, HALF], F32, name="result%d_%d" % (t, h))
                 nc.vector.tensor_tensor(result[:], turned[h][:, t, :], logs[:, t, places], ALU.add)
                 nc.sync.dma_start(out=out[t * P : (t + 1) * P, places], in_=result[:])

@@ -24,7 +24,6 @@ M_TILES = N // P
 BLOCKS = V // P
 LAST = D - 1
 HALVES = 2
-PAIRED = (5, 6)
 HALF = V // HALVES
 CAP = 30.0
 
@@ -37,7 +36,10 @@ def tile_picked_lsep_none_e_kernel(tc, xT, w1, offs, out):
 
         offsets = keep.tile([P, S // 16], U16, name="offsets")
         identity = keep.tile([P, P], F32, name="identity")
-        make_identity(nc, identity[:])
+        zero = keep.tile([P, 1], F32, name="zero")
+        nc.vector.memset(zero[:], 0.0)
+        nc.scalar.copy(out=identity[:], in_=zero[:].to_broadcast([P, P]))
+        make_identity(nc, identity[:], nomemset=True)
 
         w_grouped = keep.tile([P, N, PACK], BF16, name="w_grouped", align_bytes=64)
         w_codes = keep.tile([P, N], U32, name="w_codes", align_bytes=64)
@@ -45,11 +47,6 @@ def tile_picked_lsep_none_e_kernel(tc, xT, w1, offs, out):
 
         x_rows = xT.rearrange("(p j) t -> p j t", j=PACK)
         w_raw = keep.tile([P, PACK, N], F32, name="w_raw")
-        nc.sync.dma_start(out=w_raw[:], in_=w1.rearrange("(p j) n -> p j n", j=PACK))
-        nc.scalar.copy(out=w_grouped[:], in_=w_raw[:].rearrange("p j n -> p n j"))
-        nc.vector.quantize_mx(
-            out=w_codes[:].bitcast(FP8X4), scales=w_scales[:], in_=w_grouped[:].rearrange("p n j -> p (n j)")
-        )
         planes = []
         for j in range(PACK):
             plane = keep.tile([P, T], F32, name="plane%d" % j)
@@ -57,6 +54,8 @@ def tile_picked_lsep_none_e_kernel(tc, xT, w1, offs, out):
             nc.sync.dma_start(out=plane[:], in_=x_rows[:, j, :])
             if j == 0:
                 nc.sync.dma_start(offsets[:], offs)
+            if j == 2:
+                nc.sync.dma_start(out=w_raw[:], in_=w1.rearrange("(p j) n -> p j n", j=PACK))
 
         woven = [keep.tile([P, V, PACK], BF16, name="woven%d" % d, align_bytes=64) for d in range(D)]
 
@@ -93,9 +92,14 @@ def tile_picked_lsep_none_e_kernel(tc, xT, w1, offs, out):
         late = [keep.tile([P, 2, HALF], BF16, name="late%d" % i) for i in range(len(steps))]
         for i in [0, final] + list(range(1, final)):
             d, h = steps[i]
-            gather(2, d * V + h * HALF, HALF, late[i][:, 0, :], nc.vector if i in (0, final - 1) else nc.scalar)
-            if i not in PAIRED:
-                nc.vector.tensor_copy(out=woven[d][:, h * HALF : (h + 1) * HALF, 2], in_=late[i][:, 0, :])
+            gather(2, d * V + h * HALF, HALF, late[i][:, 0, :], nc.vector if i == 0 else nc.scalar)
+            nc.vector.tensor_copy(out=woven[d][:, h * HALF : (h + 1) * HALF, 2], in_=late[i][:, 0, :])
+            if i == 1:
+                nc.vector.tensor_copy(out=w_grouped[:], in_=w_raw[:].rearrange("p j n -> p n j"))
+            if i == 2:
+                nc.vector.quantize_mx(
+                    out=w_codes[:].bitcast(FP8X4), scales=w_scales[:], in_=w_grouped[:].rearrange("p n j -> p (n j)")
+                )
 
         packed = {}
         y = {}
@@ -190,10 +194,7 @@ def tile_picked_lsep_none_e_kernel(tc, xT, w1, offs, out):
         def weave_last(i, cols, copy=nc.vector.tensor_copy):
             d, h = steps[i]
             places = slice(h * HALF + cols.start, h * HALF + cols.stop)
-            if i in PAIRED:
-                copy(out=woven[d][:, places, 2:4], in_=late[i][:, :, cols].rearrange("p j n -> p n j"))
-            else:
-                copy(out=woven[d][:, places, 3], in_=late[i][:, 1, cols])
+            copy(out=woven[d][:, places, 3], in_=late[i][:, 1, cols])
 
         def quantize_step(i):
             d, h = steps[i]

from contextlib import ExitStack

import math

import concourse.mybir as mybir
from concourse.masks import make_identity

K, T, S, V, N = 512, 4096, 2048, 512, 256
D = S // V
FLOPS = 2 * K * N * S

F32 = mybir.dt.float32
BF16 = mybir.dt.bfloat16
U32 = mybir.dt.uint32
U16 = mybir.dt.uint16
U8 = mybir.dt.uint8
FP8X4 = mybir.dt.float8_e4m3fn_x4
ALU = mybir.AluOpType
ACT = mybir.ActivationFunctionType

P = 128
PACK = 4
M_TILES = N // P
BLOCKS = V // P
LAST = D - 1
HALVES = 2
HALF = V // HALVES
CAP = 30.0


def tile_picked_lsep_none_e_kernel(tc, xT, w1, offs, out):
    nc = tc.nc
    with ExitStack() as ctx:
        keep = ctx.enter_context(tc.tile_pool(name="keep", bufs=1))
        psum = ctx.enter_context(tc.psum_pool(name="psum", bufs=1))

        offsets = keep.tile([P, S // 16], U16, name="offsets")
        identity = keep.tile([P, P], F32, name="identity")
        zero = keep.tile([P, 1], F32, name="zero")
        nc.vector.memset(zero[:], 0.0)
        nc.scalar.copy(out=identity[:], in_=zero[:].to_broadcast([P, P]))
        make_identity(nc, identity[:], nomemset=True)

        w_grouped = keep.tile([P, N, PACK], BF16, name="w_grouped", align_bytes=64)
        w_codes = keep.tile([P, N], U32, name="w_codes", align_bytes=64)
        w_scales = keep.tile([P, N], U8, name="w_scales", align_bytes=64)

        x_rows = xT.rearrange("(p j) t -> p j t", j=PACK)
        w_raw = keep.tile([P, PACK, N], F32, name="w_raw")
        planes = []
        for j in range(PACK):
            plane = keep.tile([P, T], F32, name="plane%d" % j)
            planes.append(plane)
            nc.sync.dma_start(out=plane[:], in_=x_rows[:, j, :])
            if j == 0:
                nc.sync.dma_start(offsets[:], offs)
            if j == 2:
                nc.sync.dma_start(out=w_raw[:], in_=w1.rearrange("(p j) n -> p j n", j=PACK))

        woven = [keep.tile([P, V, PACK], BF16, name="woven%d" % d, align_bytes=64) for d in range(D)]

        def entries(first, count):
            return offsets[:, first // 16 : (first + count) // 16]

        def gather(j, first, count, target, engine):
            looked_up = planes[j][:].indirect(entries(first, count))
            if engine is nc.vector:
                nc.vector.tensor_copy(target, looked_up)
            else:
                nc.scalar.activation(target, looked_up, ACT.Copy)

        def quantize(name, source, width):
            codes = keep.tile([P, width], U32, name=name + "_codes", align_bytes=64)
            scales = keep.tile([P, width], U8, name=name + "_scales", align_bytes=64)
            nc.vector.quantize_mx(
                out=codes[:].bitcast(FP8X4), scales=scales[:], in_=source.rearrange("p n j -> p (n j)")
            )
            return codes, scales

        for j in range(2):
            rows = keep.tile([P, S], BF16, name="rows%d" % j)
            gather(j, 0, HALF, rows[:, 0:HALF], nc.vector)
            first = HALF
            for last in (V, 2 * V, 3 * V, S - HALF, S):
                gather(j, first, last - first, rows[:, first:last], nc.scalar)
                d = first // V
                begin = d * V if last < S else first
                nc.vector.tensor_copy(out=woven[d][:, begin - d * V : last - d * V, j], in_=rows[:, begin:last])
                first = last
        steps = [(d, h) for h in range(HALVES) for d in range(D)]
        final = len(steps) - 1
        late = [keep.tile([P, 2, HALF], BF16, name="late%d" % i) for i in range(len(steps))]
        for i in [0, final] + list(range(1, final)):
            d, h = steps[i]
            gather(2, d * V + h * HALF, HALF, late[i][:, 0, :], nc.vector if i == 0 else nc.scalar)
            nc.vector.tensor_copy(out=woven[d][:, h * HALF : (h + 1) * HALF, 2], in_=late[i][:, 0, :])
            if i == 1:
                nc.vector.tensor_copy(out=w_grouped[:], in_=w_raw[:].rearrange("p j n -> p n j"))
            if i == 2:
                nc.vector.quantize_mx(
                    out=w_codes[:].bitcast(FP8X4), scales=w_scales[:], in_=w_grouped[:].rearrange("p n j -> p (n j)")
                )

        packed = {}
        y = {}
        copies = {}

        def multiply(b):
            for half in range(2):
                y[b, half] = psum.tile([P, 2, N], F32, name="y%d_%d" % (b, half), tag="bank%d_%d" % (b, half))
                for i in range(2):
                    d = 2 * half + i
                    codes, scales = packed[d, b // 2]
                    first = b % 2 * P
                    nc.tensor.matmul_mx(
                        out=y[b, half][:, i, :],
                        lhsT=codes[:, first : first + P].bitcast(FP8X4),
                        lhsT_scale=scales[:, first : first + P],
                        rhs=w_codes[:].bitcast(FP8X4),
                        rhs_scale=w_scales[:],
                        start=True,
                        stop=True,
                    )
            kept = 2 if b < 2 else 1
            copies[b] = keep.tile([P, kept, N], F32, name="copy%d" % b)
            nc.scalar.copy(out=copies[b][:], in_=y[b, 0][:, 0:kept, :])

        largest = {}

        def running_max(b, step):
            before = copies[b][:, 0, :] if step == 0 else largest[b, step - 1][:]
            source = (y[b, 1][:, 0, :], y[b, 0][:, 1, :])[step]
            name = "largest%d_%d" % (b, step)
            largest[b, step] = keep.tile([P, N], F32, name=name, tag=name)
            nc.vector.tensor_tensor(largest[b, step][:], source, before, ALU.max)

        below = {}
        terms = {}
        turned = {}
        totals = {}

        def open_block(b):
            for half in range(2):
                name = "below%d_%d" % (b, half)
                below[b, half] = keep.tile([P, 2, N], F32, name=name, tag=name)

        def subtract(b, d0, d1, engine):
            if engine is nc.gpsimd:
                source = copies[b][:, d0:d1, :]
            else:
                source = y[b, d0 // 2][:, d0 % 2 : d0 % 2 + d1 - d0, :]
            shift = largest[b, 1][:].unsqueeze(1).to_broadcast([P, d1 - d0, N])
            engine.tensor_tensor(below[b, d0 // 2][:, d0 % 2 : d0 % 2 + d1 - d0, :], source, shift, ALU.subtract)

        def exponential(b, half, tag=None):
            name = "terms%d_%d" % (b, half)
            terms[b, half] = keep.tile([P, 2, N], F32, name=name, tag=tag or name)
            nc.scalar.activation(terms[b, half][:], below[b, half][:], ACT.Exp)

        def add_up(b, addends, opens, closes):
            h = b // 2
            for i, addend in enumerate(addends):
                for t in range(M_TILES):
                    if h not in totals:
                        totals[h] = psum.tile([P, M_TILES, HALF], F32, name="totals%d" % h, tag="bank%d_0" % (2 * h))
                    nc.tensor.matmul(
                        totals[h][:, t, b % 2 * P : (b % 2 + 1) * P],
                        addend[:, t * P : (t + 1) * P],
                        identity[:],
                        start=(opens and i == 0 and t == 0),
                        stop=(closes and i == len(addends) - 1 and t == M_TILES - 1),
                        is_transpose=True,
                    )

        def pair(b, half):
            return [terms[b, half][:, 0, :], terms[b, half][:, 1, :]]

        def join(b):
            joined = keep.tile([P, N], F32, name="joined%d" % b)
            nc.vector.scalar_tensor_tensor(
                out=joined[:],
                in0=terms[b, 1][:, 1, :],
                scalar=math.exp(CAP),
                in1=terms[b, 1][:, 0, :],
                op0=ALU.min,
                op1=ALU.add,
            )
            return [joined[:]]

        def gather_last(i, cols, engine):
            d, h = steps[i]
            gather(3, d * V + h * HALF + cols.start, cols.stop - cols.start, late[i][:, 1, cols], engine)

        def weave_last(i, cols, copy=nc.vector.tensor_copy):
            d, h = steps[i]
            places = slice(h * HALF + cols.start, h * HALF + cols.stop)
            copy(out=woven[d][:, places, 3], in_=late[i][:, 1, cols])

        def quantize_step(i):
            d, h = steps[i]
            packed[d, h] = quantize("piece%d_%d" % (d, h), woven[d][:, h * HALF : (h + 1) * HALF, :], HALF)

        whole = slice(0, HALF)
        gather_last(0, slice(0, P), nc.vector)
        gather_last(0, slice(P, HALF), nc.scalar)
        for i in range(1, final):
            gather_last(i, whole, nc.scalar)
        weave_last(0, slice(0, P))
        weave_last(0, slice(P, HALF))
        for i in range(final - 1):
            weave_last(i + 1, whole)
            quantize_step(i)
            if i == LAST:
                multiply(0)
                multiply(1)
        gather_last(final, whole, nc.scalar)
        weave_last(final, whole, nc.scalar.copy)
        running_max(0, 0)
        quantize_step(final - 1)
        running_max(1, 0)
        running_max(0, 1)
        quantize_step(final)
        multiply(2)
        multiply(3)
        for b in range(BLOCKS - 1):
            open_block(b)
            subtract(b, 0, 2 if b < 2 else 1, nc.gpsimd)
            subtract(b, 2, 4, nc.vector)
            running_max(b + 1, 1)
            if b == 2:
                subtract(b, 1, 2, nc.vector)
            if b + 2 < BLOCKS:
                running_max(b + 2, 0)
            exponential(b, 1)
            exponential(b, 0, "largest%d_0" % (b + 1))
            if b < 2:
                add_up(b, pair(b, 1) + pair(b, 0), True, True)
            else:
                add_up(b, pair(b, 0), True, False)
        b = BLOCKS - 1
        open_block(b)
        subtract(b, 0, 1, nc.gpsimd)
        subtract(b, 2, 4, nc.vector)
        subtract(b, 1, 2, nc.vector)
        exponential(b, 1)
        exponential(b, 0)
        add_up(b - 1, join(b - 1), False, False)
        add_up(b, join(b) + pair(b, 0), False, True)

        shifts = keep.tile([P, BLOCKS, N], F32, name="shifts", tag="copy%d" % (BLOCKS - 1))
        for b in range(BLOCKS):
            nc.vector.scalar_tensor_tensor(
                out=shifts[:, b, :], in0=y[b, 1][:, 1, :], scalar=-CAP, in1=largest[b, 1][:], op0=ALU.add, op1=ALU.max
            )
        capped = keep.tile([P, M_TILES, HALF], F32, name="capped", tag="below%d_0" % (BLOCKS - 1))
        nc.vector.tensor_scalar_min(capped[:], totals[0][:], math.exp(CAP))
        for h in range(HALVES):
            turned[h] = psum.tile([P, M_TILES, HALF], F32, name="turned%d" % h, tag="bank%d_0" % (2 * h + 1))
            for b in range(2 * h, 2 * h + 2):
                for t in range(M_TILES):
                    nc.tensor.transpose(
                        turned[h][:, t, b % 2 * P : (b % 2 + 1) * P], shifts[:, b, t * P : (t + 1) * P], identity[:]
                    )

        logs = keep.tile([P, M_TILES, V], F32, name="logs")
        for h in range(HALVES):
            for t in range(M_TILES):
                places = slice(h * HALF, (h + 1) * HALF)
                nc.scalar.activation(logs[:, t, places], (capped, totals[1])[h][:, t, :], ACT.Ln)
                result = keep.tile([P, HALF], F32, name="result%d_%d" % (t, h))
                nc.vector.tensor_tensor(result[:], turned[h][:, t, :], logs[:, t, places], ALU.add)
                nc.sync.dma_start(out=out[t * P : (t + 1) * P, places], in_=result[:])
